import numpy as np, ml_dtypes
CORES = [40,64,80,88,96,104,120,144]
N = 8
import mx_ref
BF = ml_dtypes.bfloat16
def gentries(a):
    return np.ascontiguousarray(a.reshape(8, 16, -1).transpose(0, 2, 1)).reshape(8, -1)
def gtable(e):
    e = np.asarray(e); return np.ascontiguousarray(e.reshape(8, -1, 16).transpose(0, 2, 1)).reshape(128, -1).astype(np.int32)
def gcols(t, e):
    v = np.concatenate([t.reshape(8, 16, -1, 4), np.zeros((8, 16, 1, 4), BF)], axis=2)
    return np.ascontiguousarray(np.stack([v[g][:, e[g]] for g in range(8)])).reshape(128, -1)
def tile(rs):
    return np.stack(rs, axis=2).reshape(128, -1).astype(BF)
def pick(q, e):
    c = np.concatenate([q[0].reshape(128, -1, 4), np.zeros((128, 1, 4), np.uint8)], axis=1); s = np.concatenate([q[1], np.ones((16, 1), np.uint8)], axis=1)
    return (np.ascontiguousarray(c[:, e].reshape(128, -1)), np.ascontiguousarray(s[:, e]))
def join(*qs):
    return (np.concatenate([q[0] for q in qs], axis=1), np.concatenate([q[1] for q in qs], axis=1))
def put(q, e, v):
    c, s = q[0].reshape(128, -1, 4).copy(), q[1].copy(); c[:, e] = v[0].reshape(128, -1, 4); s[:, e] = v[1]
    return (c.reshape(128, -1), s)
def pk(c, s):
    return (np.ascontiguousarray(c), mx_ref.live(s))
def emit(q):
    return q[0], q[1]
def packed(v, rng):
    q = [mx_ref.quantize(np.ascontiguousarray(v[r])) for r in range(N)]
    return np.stack([a for a, b in q]), np.stack([mx_ref.plane(b, rng) for a, b in q])
def values_of_codes():
    e, c = np.zeros((128, 128, 4), np.float32), np.zeros((128, 2, 4), np.uint8)
    e[np.arange(128), np.arange(128), 0] = 1
    c[:127, :, 0] = np.arange(256).reshape(2, 128).T[:127]
    return mx_ref.matmul(mx_ref.quantize(e.reshape(128, 512).astype(BF)), (c.reshape(128, 8), np.full((16, 2), 127, np.uint8))).T.reshape(-1).astype(np.float64)
CODE_VALUE, SCALE_VALUE = values_of_codes(), 2.0 ** (np.arange(256) - 127.0)
def decode(q):
    return (CODE_VALUE[q[0]].reshape(16, 8, -1, 4) * SCALE_VALUE[q[1]][:, None, :, None] + 0.0).reshape(128, -1).astype(np.float32)
def f(rng, *shape):
    return mx_ref.flush((rng.standard_normal(shape, dtype=np.float32) * np.exp2(rng.integers(-2, 3, shape[:-1] + (1,)))).astype(BF))
def wide(rng, *shape, cols=0):
    v = rng.standard_normal(shape, dtype=np.float32) * np.exp2(rng.integers(-12, 13, shape)).astype(np.float32)
    if cols: v *= np.repeat(np.exp2(rng.integers(-cols, cols + 1, shape[:-2] + (1, shape[-1] // 4))) * (rng.random(shape[:-2] + (1, shape[-1] // 4)) > 0.0625), 4, axis=-1).astype(np.float32)
    return mx_ref.flush(v.astype(BF))
C, S, R = 320, 32, 3
L = 3 * C + 2 * S
def flipped(t, pos):
    h, a = np.arange(3 * C), t[:, :3 * C]
    o = np.where(a < 3 * C, a, h) // 3
    low = np.minimum(a, h)
    wants = np.take_along_axis(pos, o, axis=1) != np.repeat(pos, 3, axis=1)
    least = np.min(np.where(wants, low, L).reshape(8, C, 3), axis=2)
    go = wants & (h < a) & (low == np.repeat(least, 3, axis=1)) & (low == np.take_along_axis(least, o, axis=1))
    g, i = np.nonzero(go)
    j = a[g, i]
    i1, i2 = i // 3 * 3 + (i + 1) % 3, i // 3 * 3 + (i + 2) % 3
    j1, j2 = j // 3 * 3 + (j + 1) % 3, j // 3 * 3 + (j + 2) % 3
    phi = np.tile(np.arange(L), (8, 1))
    phi[g, i2] = i1
    phi[g, j1] = i2
    phi[g, j2] = j1
    phi[g, i1] = j2
    new = np.zeros_like(t)
    np.put_along_axis(new, phi, np.take_along_axis(phi, t, axis=1), axis=1)
    return new
def anyhow(rng):
    return np.argsort(rng.random((N, 8, 3 * C)), axis=2)
def strip(rng, q):
    return np.concatenate([rng.permutation(3 * q + 2), np.stack([3 * q + 1, 3 * np.roll(q, -1)], axis=1).reshape(-1)])
def pairs(rng):
    q = rng.permutation(C).reshape(2, C // 2)
    k = np.argsort(rng.random((C // 2, 3)), axis=1)
    e = np.stack([3 * q[0][:, None] + np.arange(3), 3 * q[1][:, None] + k], axis=2)
    kept = np.ones((C // 2, 3), bool)
    kept[rng.permutation(C // 2)[:S], rng.integers(0, 3, S)] = False
    return np.concatenate([rng.permutation(e[~kept].reshape(-1)), e[kept].reshape(-1)]), q[0], q[1]
def joined(p):
    s = np.broadcast_to(3 * C + np.arange(2 * S), (N, 8, 2 * S))
    a = np.concatenate([p[:, :, :2 * S], p[:, :, 2 * S::2]], axis=2)
    b = np.concatenate([s, p[:, :, 2 * S + 1::2]], axis=2)
    e = np.zeros((N, 8, L), np.int64)
    np.put_along_axis(e, a, b, axis=2)
    np.put_along_axis(e, b, a, axis=2)
    return np.stack([gtable(k) for k in e])
def drawn(rng, x, p, u, v, w):
    c, s = packed(w, rng)
    return {"x": x, "tw": joined(p), "u": u, "v": v, "wc": c, "ws": s}
def setup_inputs(rng):
    return drawn(rng, np.array(f(rng, N, 128, 4 * C)), anyhow(rng), np.array(f(rng, N, 128, 512)), np.array(f(rng, N, 128, 512)), np.array(f(rng, N, 128, 2048)))
def setup_inputs_near(rng):
    p = anyhow(rng)
    o = rng.permutation(N)
    c = rng.integers(-1, 2, (N, 8, R, C)).astype(np.float32)
    for r in range(N):
        if o[r] == 0:
            for g in range(8): p[r, g] = strip(rng, np.arange(C))
            c[r, :, 0] = -np.abs(c[r, :, 0])
            c[r, :, 0, ::2] = 1
        if o[r] == 1: c[r] = -np.abs(c[r])
        if o[r] == 2: c[r] = 1
        if o[r] == 3:
            for g in rng.permutation(8)[:4]:
                p[r, g], a, b = pairs(rng)
                c[r, g, 0] = -np.abs(c[r, g, 0])
                c[r, g, 0, a] = 1
    x = np.array(f(rng, N, 128, 4 * C)).astype(np.float32).reshape(N, 8, 16, C, 4)
    x[:, :, :8] = 0
    x[:, :, :R, :, 0] = c * np.exp2(np.array([-30.0, -12.0, 0.0, 10.0]))[rng.integers(0, 4, (N, 8, 1, C))]
    k = np.where(rng.permutation(N) < N // 2, 2.0 ** -30, 1.0).astype(np.float32).astype(BF)
    u = np.array(f(rng, N, 128, 512)).reshape(N, 128, 128, 4)
    for g in range(8):
        for i in range(16 * g, 16 * g + R):
            u[:, :, i] = 0
            u[:, i, i, 0] = k
    w = np.array(f(rng, N, 128, 2048)).reshape(N, 8, 16, 4, 8, 16, 4)
    w[:, :, :8] = 0
    w[:, :, :, :, :, :8] = 0
    return drawn(rng, x.reshape(N, 128, 4 * C).astype(BF), p, u.reshape(N, 128, 512), np.array(f(rng, N, 128, 512)), w.reshape(N, 128, 2048))
def setup_inputs_loops(rng):
    p = anyhow(rng)
    o = rng.permutation(N)
    n = (2 * S + 5) // 6 * 2
    three = np.arange(3)
    x = np.array(f(rng, N, 128, 4 * C)).reshape(N, 128, C, 4)
    for r in range(N):
        if o[r] % 3 == 2: x[r, :, ::C - 1] = BF(-2.0 ** 26)
        for g in range(8):
            q = rng.permutation(C)
            if o[r] % 3 == 0: p[r, g] = (3 * q[:, None] + three).reshape(-1)
            if o[r] % 3 == 1:
                a, b = q[n::2], q[n + 1::2]
                k = np.argsort(rng.random((len(a), 3)), axis=1)
                e = np.stack([3 * a[:, None] + three, 3 * b[:, None] + k], axis=2)
                p[r, g] = np.concatenate([(3 * q[:n, None] + three).reshape(-1), e.reshape(-1)])
            if o[r] % 3 == 2: p[r, g] = strip(rng, q)
    return drawn(rng, x.reshape(N, 128, 4 * C), p, np.array(f(rng, N, 128, 512)), np.array(f(rng, N, 128, 512)), np.array(f(rng, N, 128, 2048)))
def setup_inputs_huge(rng):
    o = rng.permutation(N)
    x = -2.0 ** 30 * np.where(rng.random((N, 128, 4 * C)) < 0.75, 1.0, 0.5 + 0.4 * rng.random((N, 128, 4 * C)))
    x[:, 15::16] = 2.0 ** 30 * np.where(rng.random((N, 8, 4 * C)) < 0.75, -1.0, 0.5)
    s = np.argsort(rng.random((N, 128, 128)), axis=1) % 2 * 2.0 - 1.0
    s[o == 0] = 1
    s[o == 1] = -1
    u = 2.0 ** 30 * (0.75 + 0.25 * rng.random((N, 128, 128, 4))) * s[:, :, :, None]
    w = np.zeros((N, 128, 4, 128, 4), np.float32)
    i = np.arange(128)
    for b in range(4): w[:, i, b, i, b] = np.where(i % 16 == 15, -8, -24)
    return drawn(rng, x.astype(np.float32).astype(BF), anyhow(rng), u.astype(np.float32).reshape(N, 128, 512).astype(BF), np.array(f(rng, N, 128, 512)), w.reshape(N, 128, 2048).astype(BF))
def setup_inputs_spread(rng):
    d = setup_inputs(rng)
    d["x"] = np.array(wide(rng, N, 128, 4 * C, cols=6))
    return d
def check_inputs(d):
    b = []
    for k in ("x", "u", "v"):
        a = np.abs(d[k].astype(np.float32))
        if not (np.isfinite(a).all() and ((a == 0) | (a >= 2.0 ** -30) & (a <= 2.0 ** 30)).all()): b.append("a value of " + k)
    for r in range(N):
        t = gentries(d["tw"][r]).astype(np.int64)
        if ((t < 0) | (t >= L)).any(): b.append("an entry of tw")
        t = np.clip(t, 0, L - 1)
        if (np.take_along_axis(t, t, axis=1) != np.arange(L)).any(): b.append("tw: a twin's twin")
        if (t == np.arange(L)).any(): b.append("tw: a number is its own twin")
        if (t[:, 3 * C:] >= 3 * C).any(): b.append("tw: a slot's twin is a slot")
    return b
def reference(x, tw, u, v, wc, ws):
    qu = [mx_ref.quantize(u[r]) for r in range(N)]
    lay = [pk(wc[r], ws[r]) for r in range(N)]
    now = [x[r] for r in range(N)]
    twin = [gentries(tw[r]).astype(np.int64) for r in range(N)]
    for t in range(R):
        held, right, left = [], [], []
        for r in range(N):
            q = mx_ref.quantize(now[r])
            twin[r] = flipped(twin[r], mx_ref.matmul(qu[r], q)[t::16] > 0)
            held.append(decode(q))
            e = twin[r][:, 3 * C:] // 3
            right.append(mx_ref.quantize(gcols(now[r], e[:, :S])))
            left.append(mx_ref.quantize(gcols(now[r], e[:, S:])))
        for r in range(N):
            came = decode(join(left[(r + 1) % N], right[(r - 1) % N]))
            z = np.concatenate([held[r], came], axis=1).astype(BF)
            a = twin[r][:, :3 * C]
            e = np.where(a < 3 * C, a // 3, a - 2 * C)
            p = [gcols(z, e[:, k::3]).astype(np.float32) for k in range(3)]
            q = mx_ref.quantize(np.maximum(np.maximum(p[0], p[1]), p[2]).astype(BF))
            now[r] = tile([held[r][:, b::4] + np.maximum(mx_ref.matmul(pick(lay[r], np.arange(128 * b, 128 * b + 128)), q), np.float32(0.0)) * np.float32(0.015625) for b in range(4)])
    y, ot = np.zeros((N, 128, C), np.float32), np.zeros((N, 8, L), np.float32)
    oc, osc = np.zeros((N, 128, 4 * C), np.uint8), np.zeros((N, 16, C), np.uint8)
    for r in range(N):
        q = mx_ref.quantize(now[r])
        y[r] = mx_ref.matmul(mx_ref.quantize(v[r]), q)
        ot[r] = twin[r]
        oc[r], osc[r] = emit(q)
    return {"y": y, "ot": ot, "oc": oc, "osc": osc}

@@ -1,0 +1,471 @@
+from concourse.bass import DstId, RemoteDMATransfer
+from concourse.mybir import dt, AluOpType as A, ActivationFunctionType as F
+
+C, R = 320, 3
+B16, F32, U16, I32, X4, U8 = "bfloat16", "float32", "uint16", "int32", "float8_e4m3fn_x4", "uint8"
+SHARE = {"G1": (16, 20, 20), "G2": (20, 16, 16), "G3": (30, 30, 30)}
+RUNS = ((0, 192), (192, C))
+CYC, GATHER, SAME, OTHER, LOCAL, FAR = 0.001, 1.56, 0.08, 0.15, 2.0, (6.5, 5.5)
+TRIES = 1500
+
+SCRATCH = {"ps": ("psum", [128, 4096], F32)}
+PART = {}
+PLAN = {}
+
+
+def _sb(names, n, d):
+    for s in names.split():
+        SCRATCH[s] = ("sbuf", [128, n], d)
+
+
+def _parts(buf, names, n, d):
+    for i, s in enumerate(names.split()):
+        PART[s] = (buf, n * i, n)
+    _sb(buf, n * len(names.split()), d)
+
+
+_sb("X0 X1 X2", 1536, B16); _sb("X3 M0 M1 M2 p0 tm", 1280, B16); _sb("rr", 1280, F32)
+_sb("q0 q1 q2 q3 mq0 mq1 mq2", C, X4); _sb("s0 s1 s2 s3 ms0 ms1 ms2", C, U8)
+_sb("ub vb_ ct0 ct1 ct2 Cw", 512, B16); _sb("uq vq", 128, X4); _sb("us vs", 128, U8)
+_sb("wq eq", 512, X4); _sb("wsb es", 512, U8); _sb("one em", 528, B16)
+_sb("cq0 cq1 cq2 lq0 lq1 lq2", 128, X4); _sb("cs0 cs1 cs2 ls0 ls1 ls2", 128, U8)
+_sb("rq0 rq1 rq2", 64, X4); _sb("rs0 rs1 rs2", 64, U8)
+_sb("sl0 sl1 sl2 ll0 ll1 ll2", 4, U16); _sb("rl0 rl1 rl2", 2, U16)
+_sb("twi qi", 64, I32); _sb("pi", 4, I32); _sb("pf", 16, F32)
+_sb("Dw", 1536, B16); _sb("sw", 384, B16); _sb("U C2w F3w TB3", 1024, B16); _sb("W3", 1360, B16)
+_sb("G1w TB1 G2w TB2", 960, B16); _sb("TBs", C, B16); _sb("Gl TBl", 256, B16); _sb("Zw TBz", 128, B16)
+_sb("oto", 1024, F32); _sb("yb", C, F32)
+_sb("A0", 68, B16); _sb("offO offT offM", 64, U16); _sb("offX", 32, U16); _sb("offL", 24, U16)
+_parts("fa", "A1 A2 Tp vb hc K sc yy dZO dN dY n1 n2 ys lo t1 t2 t3 t4 t5 t6 t7 t8 t9 sm", 64, F32)
+_parts("ba", "Ak kc dPk dZk b1 b2 b3 b4", 64, B16); _sb("goX", 100, B16)
+for _n, _d in (("U0b", B16), ("U0c", B16), ("U0f", F32), ("U0g", F32)):
+    SCRATCH[_n] = ("sbuf", [128, 2, 2, 16], _d)
+SEMAPHORES = (["cv", "cs", "cp", "cg", "loc"] + ["d%d" % i for i in range(18)]
+              + ["%s%d" % (s, t) for s in ("ac", "al", "rc", "rl") for t in range(R)])
+
+
+def _bits(es):
+    return sum(1 << e for e in es)
+
+
+def _way(cores, r, side, topo):
+    src, dst = cores[r], cores[(r + 1 - 2 * side) % len(cores)]
+    if topo.may_write(src, dst):
+        return dst, dst
+    far = [c for c in topo.cores_of(src) if c != src and topo.may_write(c, dst)]
+    far = [c for c in far if topo.die(c) == topo.die(src)] + [c for c in far if topo.die(c) != topo.die(src)]
+    return far[side], dst
+
+
+def _engines(cores, r, topo):
+    src = cores[r]
+    ch = [topo.engines(src, _way(cores, r, s, topo)[0]) for s in (0, 1)]
+    first = 0 if len(ch[0]) <= len(ch[1]) else 1
+    out = [None, None]
+    out[first] = ch[first][:8]
+    out[1 - first] = [e for e in ch[1 - first] if e not in out[first]][:8]
+    return out
+
+
+def _to(topo, dst, src):
+    rid, pid = topo.addr(dst, src)
+    return [DstId(rid=rid, pnc=pid)]
+
+
+def relay_program(g, core, T, topo, side, dst):
+    es = topo.engines(core, dst)[:8]
+    lo = 64 - 64 * side
+    for t in range(R):
+        g.wait_ge(T.sem["rc%d" % t], 16)
+        for a, b in ((T["rq%d" % t][:, 0:64].bitcast(dt.uint8), T["lq%d" % t][:, lo:lo + 64].bitcast(dt.uint8)),
+                     (T["rs%d" % t][:, 0:64], T["ls%d" % t][:, lo:lo + 64])):
+            g.remote_dma_fused([RemoteDMATransfer(dst_ids=_to(topo, dst, core), dma_engine_mask=_bits(es),
+                                                  remote_sem=T.sem["ac%d" % t], src=a, dst=b)], local_sem=T.sem.loc)
+        g.wait_ge(T.sem["rl%d" % t], 8)
+        g.remote_dma_fused([RemoteDMATransfer(dst_ids=_to(topo, dst, core), dma_engine_mask=_bits(es), remote_sem=T.sem["al%d" % t],
+                                              src=T["rl%d" % t][:, 0:2], dst=T["ll%d" % t][:, 2 - 2 * side:4 - 2 * side])],
+                           local_sem=T.sem.loc)
+    g.wait_ge(T.sem.loc, 24 * R)
+
+
+def _order(ops):
+    seen = {}
+    for i, o in enumerate(ops):
+        deps = {}
+        for n, m, w in o["acc"]:
+            for m2, w2, j in seen.get(n, []):
+                if m & m2 and (w or w2 or (n == "ps" and ops[j]["q"] != o["q"])):
+                    deps[j] = 1
+        o["deps"] = sorted(deps)
+        o["lag"] = [(j, ops[j]["late"] + (SAME if ops[j]["q"] == o["q"] else OTHER)) for j in o["deps"]] + o["after"]
+        for n, m, w in o["acc"]:
+            seen.setdefault(n, []).append((m, w, i))
+    if "best" not in PLAN:
+        chain = [o["cost"] + o["late"] for o in ops]
+        users = [[] for o in ops]
+        for i in range(len(ops) - 1, -1, -1):
+            for j, lag in ops[i]["lag"]:
+                chain[j] = max(chain[j], chain[i] + ops[j]["cost"] + lag)
+                users[j].append(i)
+        seed, best, bias = 1, None, [0.0] * len(ops)
+        for trial in range(TRIES):
+            new = list(bias)
+            for k in range(0 if best is None else 12):
+                seed = (seed * 1103515245 + 12345) % 2147483648
+                new[(seed >> 8) % len(ops)] += ((seed >> 3) % 32 - 15.5) / 8.0
+            at = _place(ops, users, [chain[i] + new[i] for i in range(len(ops))])
+            end = max(at[i] + ops[i]["cost"] + ops[i]["late"] for i in range(len(ops)))
+            if best is None or end <= best[0]:
+                best, bias = (end, at), new
+        PLAN["best"] = best
+    at = PLAN["best"][1]
+    for i, o in enumerate(ops):
+        o["at"] = at[i]
+    return sorted(range(len(ops)), key=lambda i: (at[i], i))
+
+
+def _place(ops, users, rank):
+    left = [len(o["lag"]) for o in ops]
+    ready = [i for i in range(len(ops)) if not left[i]]
+    at, busy = [0.0] * len(ops), {}
+    while ready:
+        i = max(ready, key=lambda i: rank[i])
+        ready.remove(i)
+        o = ops[i]
+        t = max([0.0] + [at[j] + ops[j]["cost"] + lag for j, lag in o["lag"]])
+        line = busy.setdefault(o["q"], [])
+        k = len(line)
+        while k and line[k - 1][1] > t:
+            k -= 1
+        while k < len(line) and t + o["cost"] > line[k][0] + 1e-9:
+            t = max(t, line[k][1])
+            k += 1
+        line.insert(k, (t, t + o["cost"]))
+        at[i] = t
+        for j in users[i]:
+            left[j] -= 1
+            if not left[j]:
+                ready.append(j)
+    return at
+
+
+def rank_program(g, core, T, topo):
+    cores = list(T.cores)
+    rank = T.rank_of(core)
+    if rank is None:
+        for r in range(len(cores)):
+            for side in (0, 1):
+                stop, dst = _way(cores, r, side, topo)
+                if stop == core:
+                    relay_program(g, core, T, topo, side, dst)
+        return
+
+    queue = {"v": g.vector, "s": g.scalar, "p": g.tensor, "g": g, "y": g.sync}
+    ops = []
+
+    def v(name, lo=0, hi=None, step=1):
+        name, base, n = PART.get(name, (name, 0, SCRATCH.get(name, [0, [0, 0]])[1][1]))
+        lo, hi = base + lo, base + (n if hi is None else hi)
+        cols = range(lo, hi, step)
+        return (T[name][:, lo:hi:step] if step > 1 else T[name][:, lo:hi],
+                [(name, 1 << (lo // 512) if name == "ps" else _bits(cols))], len(cols), SCRATCH[name][2] in (B16, U16))
+
+    def by(win, off): return (win[0].indirect(off[0]), win[1] + off[1], 0, False)
+    def raw(x): return (x[0].bitcast(dt.uint8), x[1], 4 * x[2], False)
+
+    def call(q, fn, nout, args, cost, kw=None, kind="c", ext=None, reads=(), late=0.0):
+        kw = kw or {}
+        acc = []
+        for i, a in enumerate(list(args) + list(kw.values()) + list(reads)):
+            if isinstance(a, tuple):
+                acc += [(n, m, i < nout) for n, m in a[1]]
+        ops.append({"q": q, "fn": fn, "args": [a[0] if isinstance(a, tuple) else a for a in args], "acc": acc, "kind": kind,
+                    "kw": {k: (kw[k][0] if isinstance(kw[k], tuple) else kw[k]) for k in kw}, "cost": cost, "late": late,
+                    "ext": ext[:2] if ext else None, "after": [ext[2:]] if ext else []})
+        return len(ops) - 1
+
+    def price(o, a, x=1.0):
+        return 0.06 + o[2] * GATHER * CYC if a[2] == 0 else max(64, o[2] * x) * CYC
+
+    def tt(o, a, b, op): call("v", g.vector.tensor_tensor, 1, [o, a, b, op], price(o, a, 1.0 if a[1][0][0] == "ps" else 2.0))
+    def ts(o, a, s1, op0, s2=None, op1=None):
+        call("v", g.vector.tensor_scalar, 1, [o, a, s1, s2, op0] + ([] if op1 is None else [op1]), price(o, a))
+    def cp(o, a): call("v", g.vector.tensor_copy, 1, [o, a], price(o, a, 0.5 if o[3] and a[3] else 1.0))
+    def tr(o, a): call("v", g.vector.transpose, 1, [o, a], price(o, a, 0.5 if o[3] else 1.0))
+    def fill(o, x): call("v", g.vector.memset, 1, [o, x], price(o, o, 0.5))
+    def quant(o, s, a): call("v", g.vector.quantize_mx, 2, [o, s, a], 0.012 + 0.00027 * a[2])
+    def act(o, a, f=F.Copy, ext=None, **kw): call("s", g.scalar.activation, 1, [o, a, f], price(o, a), kw, ext=ext)
+    def mm(o, w, ws, x, xs, ext=None):
+        call("p", g.tensor.matmul_mx, 1, [o, w, ws, x, xs, True, True], (o[2] + 16) * 0.0006, ext=ext)
+    def dma(q, o, a, nbytes, reads=(), **kw):
+        call(q, queue[q].dma_start, 1, [o, a], 0.1, kw, kind="d", late=LOCAL + nbytes / 2e5, reads=reads)
+    def iota(o, pat, base, cm=0, flt=True):
+        call("g", g.iota, 1, [o, pat, base, cm], 0.13 + 2 * o[2] * CYC, {"allow_small_or_imprecise_dtypes": True} if flt else {})
+    def fb(name, r, lo=0, hi=64): return v(name, r + 16 * lo, 16 * hi, 16)
+    def bank(i, n): return v("ps", 512 * i, 512 * i + n)
+    def col(i): return v("pf", i, i + 1)
+    def halves(name): return [v(name, e, 64, 2) for e in (0, 1)]
+    def fields(name, r): return [v(name, 16 * e + r, 1024, 32) for e in (0, 1)]
+    def quad(name, b, n): return v(name, n * b, n * b + n)
+
+    def swap(u0, ins, outs):
+        for e in (0, 1):
+            tr((T[u0][:, e], [(u0, _bits(range(32 * e, 32 * e + 32)))], 32, False), ins[e])
+        for h in (0, 1):
+            tr(outs[h], (T[u0][:, :, h, :], [(u0, _bits(range(64)))], 32, False))
+
+    def turn(out, wide, t):
+        if t:
+            tr(v(out, 0, 960), v(wide, 0, 960))
+        else:
+            for k in range(3):
+                tr(v(out, C * k, C * k + C), v(wide, k, 960, 3))
+
+    def gather(out, o0, win, off, n, nv):
+        if n > nv:
+            act(v(out, o0 + 16 * nv, o0 + 16 * n), by(win, v(off, nv, n)))
+        if nv:
+            cp(v(out, o0, o0 + 16 * nv), by(win, v(off, 0, nv)))
+
+    def double(lo, src, k):
+        for h in (0, 1):
+            ts(v("offL", lo + h, lo + 8, 2), src, col(2 + h), A.mult, col(4 + 2 * k + h), A.add)
+
+    ways = [_way(cores, rank, s, topo) for s in (0, 1)]
+    eng = _engines(cores, rank, topo)
+
+    def send(pieces, sems, reads):
+        trs = []
+        for side in (0, 1):
+            stop, dst = ways[side]
+            n = 8 // len(pieces[side])
+            for i, (a, br, bd) in enumerate(pieces[side]):
+                trs.append(RemoteDMATransfer(dst_ids=_to(topo, stop, core), dma_engine_mask=_bits(eng[side][n * i:n * i + n]),
+                                             remote_sem=T.sem[sems[0] if stop == dst else sems[1]], src=a, dst=bd if stop == dst else br))
+        return call("g", g.remote_dma_fused, 0, [trs], 0.3, {"local_sem": T.sem.loc}, kind="r", reads=reads)
+
+    dma("s", v("twi"), T.tw[:], 32768)
+    dma("y", v("X0", 0, 1280), T.x[:], 327680)
+    dma("s", v("ub"), T.u[:], 131072)
+    dma("y", raw(v("wq")), T.wc[:], 262144, [v("X0", 0, 1280)])
+    dma("y", v("wsb"), T.ws[:], 65536, [v("X0", 0, 1280)])
+    dma("y", v("vb_"), T.v[:], 131072, [v("X0", 0, 1280)])
+    iota(v("pi", 0, 1), [[0, 1]], 0, 1, False)
+    fill(v("one"), 1.0)
+    call("g", g.affine_select, 1, [v("em"), v("one"), [[-1, 528]], A.is_equal, 0.0, 3, 4], 1.25)
+    for b in range(4):
+        quant(quad("eq", b, 128), quad("es", b, 128), v("em", 3 - b, 515 - b))
+    fill(v("U"), 0.0)
+    fill(v("sw", C, 384), 0.0)
+    fill(v("W3", 1344, 1360), 0.0)
+    ts(v("pi", 1, 2), v("pi", 0, 1), 31, A.bitwise_and)
+    ts(v("pi", 2, 3), v("pi", 0, 1), 15, A.bitwise_and)
+    cp(v("pf", 0, 2), v("pi", 1, 3))
+    ts(col(2), col(0), 16.0, A.is_lt)
+    ts(col(3), col(0), 16.0, A.is_ge)
+    for i, x in ((1, 3.0), (2, 1.0 / C), (3, 1.0)):
+        ts(col(12 + i), col(1), float(i), A.is_equal, x, A.mult)
+    ts(col(12), col(1), 1.0, A.is_equal, 576.0, A.mult)
+    ts(col(11), col(13), col(14), A.add, col(15), A.add)
+    for k, (real, zero) in enumerate(((192.0, 1344.0), (832.0, 960.0), (192.0, 960.0))):
+        ts(v("pf", 4 + 2 * k, 6 + 2 * k), v("pf", 2, 4), real - zero, A.mult, zero, A.add)
+    iota(v("t8", 0, 60), [[0, 3], [32, 10], [0, 2]], -192)
+    iota(v("kc", 0, 60), [[C, 3], [0, 20]], 0)
+    iota(v("sm", 32, 36), [[32, 2], [0, 2]], 128)
+    iota(v("sm", 36, 40), [[-64, 2], [16, 2]], 64)
+    iota(v("dPk", 0, 20), [[0, 20]], 2 * C)
+    iota(v("dPk", 20, 60), [[0, 40]], -C)
+    for t in range(R):
+        iota(v("X%d" % t, 1280, 1536), [[0, 256]], 0)
+    ts(v("vb", 0, 60), v("t8", 0, 60), col(0), A.add)
+    ts(v("sm", 16, 20), v("sm", 36, 40), col(1), A.add)
+    ts(v("t9", 0, 60), v("vb", 0, 60), -960.0, A.mult, 143360.0, A.add)
+    tt(v("hc", 0, 60), v("t9", 0, 60), v("kc", 0, 60), A.subtract)
+    quant(v("uq"), v("us"), v("ub"))
+    quant(v("vq"), v("vs"), v("vb_"))
+
+    cp(v("A2"), v("twi"))
+    ts(v("t1"), v("A2"), -577.0, A.add, 1.0 / 3.0, A.mult)
+    ts(v("t2"), v("A2"), -832.0, A.add)
+    ts(v("t3"), v("A2"), 960.0, A.is_ge, 640.0, A.mult)
+    cp(v("qi"), v("t1"))
+    ts(v("t4"), v("A2"), -576.0, A.add, 320.0, A.mult)
+    ts(v("t5"), v("qi"), -960.0, A.mult)
+    tt(v("A0", 0, 64), v("qi"), v("t2"), A.max)
+    tt(v("t6"), v("t4"), v("t5"), A.add)
+    ts(v("offO"), v("A0", 0, 64), 192.0, A.add)
+    tt(v("Ak"), v("t6"), v("t3"), A.max)
+    swap("U0b", halves("A0"), fields("U", 1))
+    swap("U0c", halves("Ak"), fields("U", 2))
+    tt(v("A1"), v("A0", 0, 64), v("Ak"), A.add)
+    tr(v("F3w"), v("U"))
+    turn("TB3", "F3w", 0)
+    tr(v("TB3", 960, 1024), v("F3w", 960, 1024))
+    for lo, k, f in ((0, 2, cp), (320, 0, act), (640, 1, act), (960, 2, act)):
+        f(v("W3", lo, lo + C), v("F3w", k, 960, 3))
+    cp(v("W3", 1280, 1344), v("F3w", 960, 1024))
+    ts(fb("U", 1, 60, 64), v("sm", 32, 36), col(0), A.add)
+    fill(fb("U", 2, 60, 64), 640.0)
+    ts(fb("U", 3, 60, 64), fb("U", 1, 60, 64), -2.0, A.mult, 254.0, A.add)
+    tt(v("Tp"), fb("TB3", 1), fb("TB3", 2), A.add)
+    quant(v("q0"), v("s0"), v("X0", 0, 1280))
+
+    for t in range(R):
+        for lo, hi in (RUNS if t else ((0, C),)):
+            mm(bank(4, hi - lo), v("uq"), v("us"), v("q%d" % t, lo, hi), v("s%d" % t, lo, hi))
+            act(v("sw", lo, hi), bank(4, hi - lo), F.Sign, bias=-1e-36)
+        for b in range(4):
+            mm(bank(b, C), quad("eq", b, 128), quad("es", b, 128), v("q%d" % t), v("s%d" % t))
+            act(v("Dw", 384 * b, 384 * b + C), bank(b, C))
+        ts(v("offT"), v("A1"), 192.0, A.add)
+        double(0, v("A1", 60, 64), 0)
+        ts(v("sm", 0, 4), v("A1", 60, 64), 128.0, A.is_ge, -960.0, A.mult)
+        tt(v("sm", 4, 8), v("sm", 0, 4), v("A1", 60, 64), A.add)
+        double(8, v("sm", 4, 8), 1)
+        act(v("Zw"), by(v("W3"), v("offL", 0, 8)))
+        tr(v("TBz"), v("Zw"))
+        tt(v("A0", 64, 68), v("TBz", 1, 128, 32), v("TBz", 17, 128, 32), A.add)
+        tt(v("sm", 8, 12), v("TBz", 2, 128, 32), v("TBz", 18, 128, 32), A.add)
+        tt(v("sm", 12, 16), v("sm", 8, 12), v("A0", 64, 68), A.add)
+        double(16, v("sm", 12, 16), 2)
+        for r in (1, 2):
+            act(fb("U", 3 + r, 0, 40), fb("TB3", r, 20, 60))
+            act(fb("U", 3 + r, 40, 60), fb("TB3", r, 0, 20))
+        act(v("n1", 0, 60), fb("TB3", 1, 0, 60), F.Identity, bias=143360.0, scale=-960.0)
+        tt(v("n2", 0, 60), v("n1", 0, 60), fb("TB3", 2, 0, 60), A.subtract)
+        tt(v("K", 0, 60), v("n2", 0, 60), v("hc", 0, 60), A.max)
+        act(v("b1", 0, 60), fb("TB3", 2, 0, 60), F.Abs, bias=-800.0, scale=2.0)
+        for c in range(3):
+            act(quad("dZk", c, 20), quad("b1", (c + 2) % 3, 20), F.Identity, bias=-160.0 - C * c)
+        tt(v("dZO", 20, 60), fb("TB3", 1, 0, 40), v("vb", 0, 40), A.subtract)
+        tt(v("dZO", 0, 20), fb("TB3", 1, 40, 60), v("vb", 0, 20), A.subtract)
+        tt(v("dN", 0, 40), v("Tp", 20, 60), v("Tp", 0, 40), A.subtract)
+        tt(v("dN", 40, 60), v("Tp", 0, 20), v("Tp", 40, 60), A.subtract)
+        for b in range(4):
+            ts(quad("offX", b, 8), v("A0", 60, 68), 4.0, A.mult, 768.0 + b, A.add)
+            act(v("ct%d" % t, b, 512, 4), by(v("X%d" % t), quad("offX", b, 8)))
+        quant(v("cq%d" % t), v("cs%d" % t), v("ct%d" % t))
+        for src, rel, land, f in (("cq", "rq", "lq", lambda a: a.bitcast(dt.uint8)), ("cs", "rs", "ls", lambda a: a)):
+            sent = send([[(f(T["%s%d" % (src, t)][:, 32 * side + 64 * i:32 * side + 64 * i + 32]),
+                           f(T["%s%d" % (rel, t)][:, 32 * i:32 * i + 32]),
+                           f(T["%s%d" % (land, t)][:, 64 - 64 * side + 32 * i:96 - 64 * side + 32 * i])) for i in (0, 1)]
+                         for side in (0, 1)], ("ac%d" % t, "rc%d" % t), [v("%s%d" % (src, t))])
+        gather("G1w", 0, v("sw"), "offO", 60, SHARE["G1"][t])
+        tr(v("TBs"), v("sw", 0, C))
+        for k in range(3):
+            tt(quad("sc", k, 20), fb("TBs", t, 0, 20), quad("K", k, 20), A.mult)
+        turn("TB1", "G1w", t)
+        tt(v("yy", 0, 60), fb("TB1", t, 0, 60), v("sc", 0, 60), A.mult)
+        tt(v("lo", 0, 20), v("yy", 0, 20), v("yy", 20, 40), A.min)
+        ts(v("lo", 20, 40), v("yy", 40, 60), -1.0, A.min)
+        tt(v("lo", 40, 60), v("lo", 0, 20), v("lo", 20, 40), A.min)
+        for k in range(3):
+            tt(fb("U", 0, 20 * k, 20 * k + 20), quad("yy", k, 20), v("lo", 40, 60), A.is_equal)
+        tr(v("C2w"), v("U"))
+        act(v("Gl", 128, 256), by(v("C2w"), v("offL", 16, 24)), F.Identity, scale=32.0)
+        cp(v("Gl", 0, 128), by(v("C2w"), v("offL", 8, 16)))
+        tr(v("TBl"), v("Gl"))
+        tt(v("sm", 24, 32), v("TBl", 0, 256, 32), v("TBl", 16, 256, 32), A.add)
+        for c in range(4):
+            ts(v("sl%d" % t, c, c + 1), v("sm", 24 + c, 25 + c), v("sm", 28 + c, 29 + c), A.mult, v("sm", 16 + c, 17 + c), A.add)
+        told = send([[(T["sl%d" % t][:, 2 * side:2 * side + 2], T["rl%d" % t][:, 0:2], T["ll%d" % t][:, 2 - 2 * side:4 - 2 * side])]
+                     for side in (0, 1)], ("al%d" % t, "rl%d" % t), [v("sl%d" % t)])
+        ops[told]["after"].append((sent, 0.0))
+        gather("G2w", 0, v("C2w"), "offT", 60, SHARE["G2"][t])
+        turn("TB2", "G2w", t)
+        tt(v("goX", 20, 80), fb("TB2", 0, 0, 60), fb("U", 0, 0, 60), A.mult)
+        tt(v("goX", 0, 20), fb("TB2", 0, 40, 60), fb("U", 0, 40, 60), A.mult)
+        tt(v("goX", 80, 100), fb("TB2", 0, 0, 20), fb("U", 0, 0, 20), A.mult)
+        tt(v("ys", 0, 40), fb("TB2", 4, 20, 60), fb("TB2", 5, 20, 60), A.add)
+        tt(v("ys", 40, 60), fb("TB2", 4, 0, 20), fb("TB2", 5, 0, 20), A.add)
+        tt(v("dY", 0, 60), v("ys", 0, 60), v("Tp", 0, 60), A.subtract)
+        gp, gn = v("goX", 0, 60), v("goX", 40, 100)
+        tt(v("t1", 0, 60), gp, v("dZO", 0, 60), A.mult)
+        tt(v("b2", 0, 60), gn, v("dPk", 0, 60), A.mult)
+        tt(v("b3", 0, 60), gp, v("dZk", 0, 60), A.mult)
+        tt(v("t4", 0, 60), gp, v("dN", 0, 60), A.mult)
+        tt(v("t5", 0, 60), gn, v("dY", 0, 60), A.mult)
+        tt(fb("U", 1, 0, 60), v("t1", 0, 60), v("vb", 0, 60), A.add)
+        tt(v("b4", 0, 60), v("b2", 0, 60), v("kc", 0, 60), A.add)
+        tt(v("t7", 0, 60), v("t4", 0, 60), v("Tp", 0, 60), A.add)
+        tt(fb("U", 2, 0, 60), v("b4", 0, 60), v("b3", 0, 60), A.add)
+        tt(v("Tp", 0, 60), v("t7", 0, 60), v("t5", 0, 60), A.add)
+        tr(v("F3w"), v("U"))
+        swap("U0f", halves("Tp"), halves("A2"))
+        ts(v("offM"), v("A2"), 192.0, A.add)
+        gather("W3", C, v("F3w"), "offM", 64, SHARE["G3"][t])
+        tr(v("TB3"), v("W3", C, 1344))
+        swap("U0b", fields("TB3", 1), halves("A0"))
+        ts(v("offO"), v("A0", 0, 64), 192.0, A.add)
+        if t < R - 1:
+            act(v("W3", 0, C), v("W3", 960, 1280))
+            tt(v("Tp"), fb("TB3", 1), fb("TB3", 2), A.add)
+            swap("U0g", halves("Tp"), halves("A1"))
+        else:
+            for k in range(3):
+                act(v("oto", k, 960, 3), v("W3", C + C * k, 640 + C * k), F.Identity, bias=col(12), scale=col(11))
+            act(v("oto", 960, 1024), v("W3", 1280, 1344), F.Identity, bias=col(12), scale=col(11))
+            ot = (T.ot[:], [("ot", 1)])
+            dma("y", ot, (T.oto[1:128:16, :], v("oto")[1]), 32768)
+            for r in (2, 3):
+                dma("g", ot, (T.oto[r:128:16, :], v("oto")[1]), 200000, accum_op=A.add)
+        for b in range(4):
+            mm(bank(4 + b, 128), quad("eq", b, 128), quad("es", b, 128), v("lq%d" % t), v("ls%d" % t),
+               ext=("ac%d" % t, 32, sent, FAR[0] + (3.0 if t == 0 else 0.0)))
+            act(quad("Cw", b, 128), bank(4 + b, 128))
+            act(v("Dw", 384 * b + C, 384 * b + 384), by(quad("Cw", b, 128), (T["ll%d" % t][:, 0:4], [])),
+                ext=("al%d" % t, 16, told, FAR[1]))
+        for lo, hi in RUNS:
+            n, a, z = hi - lo, lo // 16, hi // 16
+            for b in range(4):
+                win, p0, tm = quad("Dw", b, 384), v("p0", C * b + lo, C * b + hi), v("tm", C * b + lo, C * b + hi)
+                act(p0, by(win, v("offO", a, z)))
+                tt(tm, by(win, v("offO", 20 + a, 20 + z)), p0, A.max)
+                tt(v("M%d" % t, 4 * lo + b, 4 * hi, 4), by(win, v("offO", 40 + a, 40 + z)), tm, A.max)
+            mq, ms = v("mq%d" % t, lo, hi), v("ms%d" % t, lo, hi)
+            quant(mq, ms, v("M%d" % t, 4 * lo, 4 * hi))
+            for b in range(4):
+                rr = v("rr", C * b + lo, C * b + hi)
+                mm(bank(4 + b, n), quad("wq", b, 128), quad("wsb", b, 128), mq, ms)
+                act(rr, bank(4 + b, n), F.Relu, scale=0.015625)
+                tt(v("X%d" % (t + 1), 4 * lo + b, 4 * hi, 4), v("ps", 512 * b + lo, 512 * b + hi), rr, A.add)
+            q, s = v("q%d" % (t + 1), lo, hi), v("s%d" % (t + 1), lo, hi)
+            quant(q, s, v("X%d" % (t + 1), 4 * lo, 4 * hi))
+            if t == R - 1:
+                mm(bank(4, n), v("vq"), v("vs"), q, s)
+                (cp if hi == C else act)(v("yb", lo, hi), bank(4, n))
+                dma("s" if hi == C else "y", T.y[:, lo:hi], v("yb", lo, hi), 512 * n)
+                dma("y", T.oc[:, 4 * lo:4 * hi], raw(q), 512 * n)
+    for k in range(4):
+        dma("s" if k < 2 else "y", T.osc[4 * k:4 * k + 4, :], (T.s3[32 * k:32 * k + 4, :], v("s3")[1]), 1280)
+
+    known = {q: {} for q in queue}
+    count = {}
+
+    def wait(q, sem, n, more):
+        if known[q].get(sem, 0) < n:
+            queue[q].wait_ge(T.sem[sem], n)
+            known[q][sem] = n
+            for s in more:
+                known[q][s] = max(known[q].get(s, 0), more[s])
+
+    ndma, nsent = 0, 0
+    for i in _order(ops):
+        o = ops[i]
+        q = o["q"]
+        for j in sorted(o["deps"], key=lambda j: -ops[j]["at"]):
+            wait(q, ops[j]["sem"], ops[j]["cnt"], ops[j]["known"])
+        if o["ext"]:
+            wait(q, o["ext"][0], o["ext"][1], {})
+        ins = o["fn"](*o["args"], **o["kw"])
+        if o["kind"] == "r":
+            nsent += 16
+            continue
+        sem, inc = ("c" + q, 1) if o["kind"] == "c" else ("d%d" % ndma, 16)
+        ndma += o["kind"] == "d"
+        count[sem] = count.get(sem, 0) + inc
+        ins.then_inc(T.sem[sem], inc)
+        o["sem"], o["cnt"], o["known"] = sem, count[sem], dict(known[q])
+    g.wait_ge(T.sem.loc, nsent)
+    for sem in count:
+        wait("g", sem, count[sem], {})

@@ -3,11 +3,10 @@ from concourse.mybir import dt, AluOpType as A, ActivationFunctionType as F
 
 C, R = 320, 3
 B16, F32, U16, I32, X4, U8 = "bfloat16", "float32", "uint16", "int32", "float8_e4m3fn_x4", "uint8"
-SHARE = {"G1": (16, 20, 20), "G2": (20, 16, 16), "G3": (30, 30, 30)}
+SHARE = {"G1": 16, "G2": 14, "G3": 30}
 RUNS = ((0, 192), (192, C))
-CYC, GATHER, SAME, OTHER, LOCAL, FAR = 0.001, 1.56, 0.08, 0.15, 2.0, (6.5, 5.5)
-TRIES = 1500
-
+CYC, FIXED, GATHER, SAME, OTHER, LOCAL, FAR = 0.001, 0.03, 1.7, 0.1, 0.2, 2.0, ((9.5, 9.0, 9.0), 6.5)
+TRIES, SHAKE = 3000, 30
 SCRATCH = {"ps": ("psum", [128, 4096], F32)}
 PART = {}
 PLAN = {}
@@ -31,13 +30,13 @@ _sb("wq eq", 512, X4); _sb("wsb es", 512, U8); _sb("one em", 528, B16)
 _sb("cq0 cq1 cq2 lq0 lq1 lq2", 128, X4); _sb("cs0 cs1 cs2 ls0 ls1 ls2", 128, U8)
 _sb("rq0 rq1 rq2", 64, X4); _sb("rs0 rs1 rs2", 64, U8)
 _sb("sl0 sl1 sl2 ll0 ll1 ll2", 4, U16); _sb("rl0 rl1 rl2", 2, U16)
-_sb("twi qi", 64, I32); _sb("pi", 4, I32); _sb("pf", 16, F32)
-_sb("Dw", 1536, B16); _sb("sw", 384, B16); _sb("U C2w F3w TB3", 1024, B16); _sb("W3", 1360, B16)
+_sb("twi qi", 64, I32); _sb("pi", 4, I32); _sb("pf", 18, F32)
+_sb("Dw", 1536, B16); _sb("sw", 384, B16); _sb("U C2w TB3", 1024, B16); _sb("F3w", 1040, B16); _sb("W3", 1360, B16)
 _sb("G1w TB1 G2w TB2", 960, B16); _sb("TBs", C, B16); _sb("Gl TBl", 256, B16); _sb("Zw TBz", 128, B16)
 _sb("oto", 1024, F32); _sb("yb", C, F32)
-_sb("A0", 68, B16); _sb("offO offT offM", 64, U16); _sb("offX", 32, U16); _sb("offL", 24, U16)
-_parts("fa", "A1 A2 Tp vb hc K sc yy dZO dN dY n1 n2 ys lo t1 t2 t3 t4 t5 t6 t7 t8 t9 sm", 64, F32)
-_parts("ba", "Ak kc dPk dZk b1 b2 b3 b4", 64, B16); _sb("goX", 100, B16)
+_sb("A0", 68, B16); _sb("offO offT offM", 64, U16); _sb("offL", 56, U16)
+_parts("fa", "A1 A2 Tp vb hc K sc dZO dN dY n1 n2 ys lo t1 t2 t3 t4 t5 t6 t7 t8 t9 sm fl", 64, F32)
+_parts("ba", "Ak kc dPk dZk b1 b2 b3 b4", 64, B16); _sb("goX", 100, B16); _sb("yy", 100, F32)
 for _n, _d in (("U0b", B16), ("U0c", B16), ("U0f", F32), ("U0g", F32)):
     SCRATCH[_n] = ("sbuf", [128, 2, 2, 16], _d)
 SEMAPHORES = (["cv", "cs", "cp", "cg", "loc"] + ["d%d" % i for i in range(18)]
@@ -101,22 +100,27 @@ def _order(ops):
         for n, m, w in o["acc"]:
             seen.setdefault(n, []).append((m, w, i))
     if "best" not in PLAN:
-        chain = [o["cost"] + o["late"] for o in ops]
-        users = [[] for o in ops]
-        for i in range(len(ops) - 1, -1, -1):
-            for j, lag in ops[i]["lag"]:
-                chain[j] = max(chain[j], chain[i] + ops[j]["cost"] + lag)
-                users[j].append(i)
-        seed, best, bias = 1, None, [0.0] * len(ops)
+        n = len(ops)
+        cost, que = [o["cost"] for o in ops], [o["q"] for o in ops]
+        ahead = [o["lag"] for o in ops]
+        behind = [[] for o in ops]
+        rank = [o["cost"] + o["late"] for o in ops]
+        for i in range(n - 1, -1, -1):
+            for j, lag in ahead[i]:
+                rank[j] = max(rank[j], rank[i] + cost[j] + lag)
+                behind[j].append((i, lag))
+        seed, best = 1, None
         for trial in range(TRIES):
-            new = list(bias)
-            for k in range(0 if best is None else 12):
-                seed = (seed * 1103515245 + 12345) % 2147483648
-                new[(seed >> 8) % len(ops)] += ((seed >> 3) % 32 - 15.5) / 8.0
-            at = _place(ops, users, [chain[i] + new[i] for i in range(len(ops))])
-            end = max(at[i] + ops[i]["cost"] + ops[i]["late"] for i in range(len(ops)))
+            at = _place(cost, que, ahead, behind, rank, [0.0] * n)
+            end = max(at[i] + cost[i] + ops[i]["late"] for i in range(n))
             if best is None or end <= best[0]:
-                best, bias = (end, at), new
+                best = (end, at)
+            at = list(best[1])
+            for k in range(SHAKE):
+                seed = (seed * 1103515245 + 12345) % 2147483648
+                at[(seed >> 8) % n] += ((seed >> 3) % 32 - 15.5) / 16.0
+            back = _place(cost, que, behind, ahead, [at[i] + cost[i] for i in range(n)], [o["late"] for o in ops])
+            rank = [back[i] + cost[i] for i in range(n)]
         PLAN["best"] = best
     at = PLAN["best"][1]
     for i, o in enumerate(ops):
@@ -124,25 +128,24 @@ def _order(ops):
     return sorted(range(len(ops)), key=lambda i: (at[i], i))
 
 
-def _place(ops, users, rank):
-    left = [len(o["lag"]) for o in ops]
-    ready = [i for i in range(len(ops)) if not left[i]]
-    at, busy = [0.0] * len(ops), {}
+def _place(cost, que, ahead, behind, rank, first):
+    left = [len(a) for a in ahead]
+    ready = [i for i in range(len(cost)) if not left[i]]
+    at, busy = [0.0] * len(cost), {}
     while ready:
         i = max(ready, key=lambda i: rank[i])
         ready.remove(i)
-        o = ops[i]
-        t = max([0.0] + [at[j] + ops[j]["cost"] + lag for j, lag in o["lag"]])
-        line = busy.setdefault(o["q"], [])
+        t = max([first[i]] + [at[j] + cost[j] + lag for j, lag in ahead[i]])
+        line = busy.setdefault(que[i], [])
         k = len(line)
         while k and line[k - 1][1] > t:
             k -= 1
-        while k < len(line) and t + o["cost"] > line[k][0] + 1e-9:
+        while k < len(line) and t + cost[i] > line[k][0] + 1e-9:
             t = max(t, line[k][1])
             k += 1
-        line.insert(k, (t, t + o["cost"]))
+        line.insert(k, (t, t + cost[i]))
         at[i] = t
-        for j in users[i]:
+        for j, lag in behind[i]:
             left[j] -= 1
             if not left[j]:
                 ready.append(j)
@@ -159,7 +162,6 @@ def rank_program(g, core, T, topo):
                 if stop == core:
                     relay_program(g, core, T, topo, side, dst)
         return
-
     queue = {"v": g.vector, "s": g.scalar, "p": g.tensor, "g": g, "y": g.sync}
     ops = []
 
@@ -185,7 +187,7 @@ def rank_program(g, core, T, topo):
         return len(ops) - 1
 
     def price(o, a, x=1.0):
-        return 0.06 + o[2] * GATHER * CYC if a[2] == 0 else max(64, o[2] * x) * CYC
+        return FIXED + (0.05 + o[2] * GATHER * CYC if a[2] == 0 else max(64, o[2] * x) * CYC)
 
     def tt(o, a, b, op): call("v", g.vector.tensor_tensor, 1, [o, a, b, op], price(o, a, 1.0 if a[1][0][0] == "ps" else 2.0))
     def ts(o, a, s1, op0, s2=None, op1=None):
@@ -193,7 +195,7 @@ def rank_program(g, core, T, topo):
     def cp(o, a): call("v", g.vector.tensor_copy, 1, [o, a], price(o, a, 0.5 if o[3] and a[3] else 1.0))
     def tr(o, a): call("v", g.vector.transpose, 1, [o, a], price(o, a, 0.5 if o[3] else 1.0))
     def fill(o, x): call("v", g.vector.memset, 1, [o, x], price(o, o, 0.5))
-    def quant(o, s, a): call("v", g.vector.quantize_mx, 2, [o, s, a], 0.012 + 0.00027 * a[2])
+    def quant(o, s, a): call("v", g.vector.quantize_mx, 2, [o, s, a], FIXED + 0.012 + 0.27 * CYC * a[2])
     def act(o, a, f=F.Copy, ext=None, **kw): call("s", g.scalar.activation, 1, [o, a, f], price(o, a), kw, ext=ext)
     def mm(o, w, ws, x, xs, ext=None):
         call("p", g.tensor.matmul_mx, 1, [o, w, ws, x, xs, True, True], (o[2] + 16) * 0.0006, ext=ext)
@@ -222,14 +224,12 @@ def rank_program(g, core, T, topo):
                 tr(v(out, C * k, C * k + C), v(wide, k, 960, 3))
 
     def gather(out, o0, win, off, n, nv):
-        if n > nv:
-            act(v(out, o0 + 16 * nv, o0 + 16 * n), by(win, v(off, nv, n)))
-        if nv:
-            cp(v(out, o0, o0 + 16 * nv), by(win, v(off, 0, nv)))
+        act(v(out, o0 + 16 * nv, o0 + 16 * n), by(win, v(off, nv, n)))
+        cp(v(out, o0, o0 + 16 * nv), by(win, v(off, 0, nv)))
 
     def double(lo, src, k):
         for h in (0, 1):
-            ts(v("offL", lo + h, lo + 8, 2), src, col(2 + h), A.mult, col(4 + 2 * k + h), A.add)
+            act(v("fl", lo + h, lo + 8, 2), src, F.Identity, scale=col(2 + h), bias=col(4 + 2 * k + h))
 
     ways = [_way(cores, rank, s, topo) for s in (0, 1)]
     eng = _engines(cores, rank, topo)
@@ -258,16 +258,16 @@ def rank_program(g, core, T, topo):
     fill(v("U"), 0.0)
     fill(v("sw", C, 384), 0.0)
     fill(v("W3", 1344, 1360), 0.0)
+    fill(v("F3w", 1024, 1040), 0.0)
     ts(v("pi", 1, 2), v("pi", 0, 1), 31, A.bitwise_and)
     ts(v("pi", 2, 3), v("pi", 0, 1), 15, A.bitwise_and)
     cp(v("pf", 0, 2), v("pi", 1, 3))
     ts(col(2), col(0), 16.0, A.is_lt)
     ts(col(3), col(0), 16.0, A.is_ge)
-    for i, x in ((1, 3.0), (2, 1.0 / C), (3, 1.0)):
-        ts(col(12 + i), col(1), float(i), A.is_equal, x, A.mult)
-    ts(col(12), col(1), 1.0, A.is_equal, 576.0, A.mult)
-    ts(col(11), col(13), col(14), A.add, col(15), A.add)
-    for k, (real, zero) in enumerate(((192.0, 1344.0), (832.0, 960.0), (192.0, 960.0))):
+    ts(col(13), col(1), 1.0, A.is_equal, 2.0, A.mult)
+    ts(col(12), col(13), 288.0, A.mult)
+    ts(col(11), col(13), 1.0, A.add)
+    for k, real, zero in ((0, 192.0, 1344.0), (1, 832.0, 960.0), (2, 192.0, 960.0), (6, -1.0, 1024.0)):
         ts(v("pf", 4 + 2 * k, 6 + 2 * k), v("pf", 2, 4), real - zero, A.mult, zero, A.add)
     iota(v("t8", 0, 60), [[0, 3], [32, 10], [0, 2]], -192)
     iota(v("kc", 0, 60), [[C, 3], [0, 20]], 0)
@@ -283,7 +283,6 @@ def rank_program(g, core, T, topo):
     tt(v("hc", 0, 60), v("t9", 0, 60), v("kc", 0, 60), A.subtract)
     quant(v("uq"), v("us"), v("ub"))
     quant(v("vq"), v("vs"), v("vb_"))
-
     cp(v("A2"), v("twi"))
     ts(v("t1"), v("A2"), -577.0, A.add, 1.0 / 3.0, A.mult)
     ts(v("t2"), v("A2"), -832.0, A.add)
@@ -298,15 +297,12 @@ def rank_program(g, core, T, topo):
     swap("U0b", halves("A0"), fields("U", 1))
     swap("U0c", halves("Ak"), fields("U", 2))
     tt(v("A1"), v("A0", 0, 64), v("Ak"), A.add)
-    tr(v("F3w"), v("U"))
+    tr(v("F3w", 0, 1024), v("U"))
     turn("TB3", "F3w", 0)
     tr(v("TB3", 960, 1024), v("F3w", 960, 1024))
-    for lo, k, f in ((0, 2, cp), (320, 0, act), (640, 1, act), (960, 2, act)):
-        f(v("W3", lo, lo + C), v("F3w", k, 960, 3))
-    cp(v("W3", 1280, 1344), v("F3w", 960, 1024))
     ts(fb("U", 1, 60, 64), v("sm", 32, 36), col(0), A.add)
     fill(fb("U", 2, 60, 64), 640.0)
-    ts(fb("U", 3, 60, 64), fb("U", 1, 60, 64), -2.0, A.mult, 254.0, A.add)
+    ts(fb("U", 3, 60, 64), fb("U", 1, 60, 64), -2.0, A.mult, 256.0, A.add)
     tt(v("Tp"), fb("TB3", 1), fb("TB3", 2), A.add)
     quant(v("q0"), v("s0"), v("X0", 0, 1280))
 
@@ -318,11 +314,17 @@ def rank_program(g, core, T, topo):
             mm(bank(b, C), quad("eq", b, 128), quad("es", b, 128), v("q%d" % t), v("s%d" % t))
             act(v("Dw", 384 * b, 384 * b + C), bank(b, C))
         ts(v("offT"), v("A1"), 192.0, A.add)
-        double(0, v("A1", 60, 64), 0)
+        if t:
+            double(0, v("A1", 60, 64), 0)
+        else:
+            ts(v("sm", 48, 52), v("Ak", 60, 64), 0.0, A.is_equal, 3.0, A.mult)
+            tt(v("sm", 52, 56), v("sm", 48, 52), v("A2", 60, 64), A.add)
+            double(0, v("sm", 52, 56), 6)
         ts(v("sm", 0, 4), v("A1", 60, 64), 128.0, A.is_ge, -960.0, A.mult)
         tt(v("sm", 4, 8), v("sm", 0, 4), v("A1", 60, 64), A.add)
         double(8, v("sm", 4, 8), 1)
-        act(v("Zw"), by(v("W3"), v("offL", 0, 8)))
+        cp(v("offL", 0, 8), v("fl", 0, 8))
+        act(v("Zw"), by(v("W3" if t else "F3w"), v("offL", 0, 8)))
         tr(v("TBz"), v("Zw"))
         tt(v("A0", 64, 68), v("TBz", 1, 128, 32), v("TBz", 17, 128, 32), A.add)
         tt(v("sm", 8, 12), v("TBz", 2, 128, 32), v("TBz", 18, 128, 32), A.add)
@@ -332,35 +334,39 @@ def rank_program(g, core, T, topo):
             act(fb("U", 3 + r, 0, 40), fb("TB3", r, 20, 60))
             act(fb("U", 3 + r, 40, 60), fb("TB3", r, 0, 20))
         act(v("n1", 0, 60), fb("TB3", 1, 0, 60), F.Identity, bias=143360.0, scale=-960.0)
-        tt(v("n2", 0, 60), v("n1", 0, 60), fb("TB3", 2, 0, 60), A.subtract)
-        tt(v("K", 0, 60), v("n2", 0, 60), v("hc", 0, 60), A.max)
+        tt(v("t3", 0, 60), v("n1", 0, 60), fb("TB3", 2, 0, 60), A.subtract)
+        tt(v("K", 0, 60), v("t3", 0, 60), v("hc", 0, 60), A.max)
         act(v("b1", 0, 60), fb("TB3", 2, 0, 60), F.Abs, bias=-800.0, scale=2.0)
         for c in range(3):
             act(quad("dZk", c, 20), quad("b1", (c + 2) % 3, 20), F.Identity, bias=-160.0 - C * c)
-        tt(v("dZO", 20, 60), fb("TB3", 1, 0, 40), v("vb", 0, 40), A.subtract)
-        tt(v("dZO", 0, 20), fb("TB3", 1, 40, 60), v("vb", 0, 20), A.subtract)
-        tt(v("dN", 0, 40), v("Tp", 20, 60), v("Tp", 0, 40), A.subtract)
-        tt(v("dN", 40, 60), v("Tp", 0, 20), v("Tp", 40, 60), A.subtract)
+        act(v("n2", 20, 60), fb("TB3", 1, 0, 40))
+        act(v("n2", 0, 20), fb("TB3", 1, 40, 60))
+        tt(v("dZO", 0, 60), v("n2", 0, 60), v("vb", 0, 60), A.subtract)
+        act(v("t2", 0, 40), v("Tp", 20, 60))
+        act(v("t2", 40, 60), v("Tp", 0, 20))
+        tt(v("dN", 0, 60), v("t2", 0, 60), v("Tp", 0, 60), A.subtract)
         for b in range(4):
-            ts(quad("offX", b, 8), v("A0", 60, 68), 4.0, A.mult, 768.0 + b, A.add)
-            act(v("ct%d" % t, b, 512, 4), by(v("X%d" % t), quad("offX", b, 8)))
+            act(v("fl", 24 + 8 * b, 32 + 8 * b), v("A0", 60, 68), F.Identity, scale=4.0, bias=768.0 + b)
+        cp(v("offL", 24, 56), v("fl", 24, 56))
+        cp(v("offL", 8, 24), v("fl", 8, 24))
+        for b in range(4):
+            act(v("ct%d" % t, b, 512, 4), by(v("X%d" % t), quad("offL", 3 + b, 8)))
         quant(v("cq%d" % t), v("cs%d" % t), v("ct%d" % t))
         for src, rel, land, f in (("cq", "rq", "lq", lambda a: a.bitcast(dt.uint8)), ("cs", "rs", "ls", lambda a: a)):
             sent = send([[(f(T["%s%d" % (src, t)][:, 32 * side + 64 * i:32 * side + 64 * i + 32]),
                            f(T["%s%d" % (rel, t)][:, 32 * i:32 * i + 32]),
                            f(T["%s%d" % (land, t)][:, 64 - 64 * side + 32 * i:96 - 64 * side + 32 * i])) for i in (0, 1)]
                          for side in (0, 1)], ("ac%d" % t, "rc%d" % t), [v("%s%d" % (src, t))])
-        gather("G1w", 0, v("sw"), "offO", 60, SHARE["G1"][t])
+        gather("G1w", 0, v("sw"), "offO", 60, SHARE["G1"])
         tr(v("TBs"), v("sw", 0, C))
         for k in range(3):
             tt(quad("sc", k, 20), fb("TBs", t, 0, 20), quad("K", k, 20), A.mult)
         turn("TB1", "G1w", t)
         tt(v("yy", 0, 60), fb("TB1", t, 0, 60), v("sc", 0, 60), A.mult)
-        tt(v("lo", 0, 20), v("yy", 0, 20), v("yy", 20, 40), A.min)
-        ts(v("lo", 20, 40), v("yy", 40, 60), -1.0, A.min)
-        tt(v("lo", 40, 60), v("lo", 0, 20), v("lo", 20, 40), A.min)
-        for k in range(3):
-            tt(fb("U", 0, 20 * k, 20 * k + 20), quad("yy", k, 20), v("lo", 40, 60), A.is_equal)
+        tt(v("yy", 60, 100), fb("TB1", t, 0, 40), v("sc", 0, 40), A.mult)
+        tt(v("lo", 0, 60), v("yy", 20, 80), v("yy", 40, 100), A.min)
+        ts(v("t9", 0, 60), v("lo", 0, 60), -1.0, A.min)
+        tt(fb("U", 0, 0, 60), v("yy", 0, 60), v("t9", 0, 60), A.is_lt)
         tr(v("C2w"), v("U"))
         act(v("Gl", 128, 256), by(v("C2w"), v("offL", 16, 24)), F.Identity, scale=32.0)
         cp(v("Gl", 0, 128), by(v("C2w"), v("offL", 8, 16)))
@@ -371,7 +377,7 @@ def rank_program(g, core, T, topo):
         told = send([[(T["sl%d" % t][:, 2 * side:2 * side + 2], T["rl%d" % t][:, 0:2], T["ll%d" % t][:, 2 - 2 * side:4 - 2 * side])]
                      for side in (0, 1)], ("al%d" % t, "rl%d" % t), [v("sl%d" % t)])
         ops[told]["after"].append((sent, 0.0))
-        gather("G2w", 0, v("C2w"), "offT", 60, SHARE["G2"][t])
+        gather("G2w", 0, v("C2w"), "offT", 60, SHARE["G2"])
         turn("TB2", "G2w", t)
         tt(v("goX", 20, 80), fb("TB2", 0, 0, 60), fb("U", 0, 0, 60), A.mult)
         tt(v("goX", 0, 20), fb("TB2", 0, 40, 60), fb("U", 0, 40, 60), A.mult)
@@ -390,10 +396,12 @@ def rank_program(g, core, T, topo):
         tt(v("t7", 0, 60), v("t4", 0, 60), v("Tp", 0, 60), A.add)
         tt(fb("U", 2, 0, 60), v("b4", 0, 60), v("b3", 0, 60), A.add)
         tt(v("Tp", 0, 60), v("t7", 0, 60), v("t5", 0, 60), A.add)
-        tr(v("F3w"), v("U"))
+        if t == R - 1:
+            ts(fb("U", 3, 0, 60), fb("U", 2, 0, 60), 1.0 / C, A.mult)
+        tr(v("F3w", 0, 1024), v("U"))
         swap("U0f", halves("Tp"), halves("A2"))
         ts(v("offM"), v("A2"), 192.0, A.add)
-        gather("W3", C, v("F3w"), "offM", 64, SHARE["G3"][t])
+        gather("W3", C, v("F3w", 0, 1024), "offM", 64, SHARE["G3"])
         tr(v("TB3"), v("W3", C, 1344))
         swap("U0b", fields("TB3", 1), halves("A0"))
         ts(v("offO"), v("A0", 0, 64), 192.0, A.add)
@@ -406,12 +414,11 @@ def rank_program(g, core, T, topo):
                 act(v("oto", k, 960, 3), v("W3", C + C * k, 640 + C * k), F.Identity, bias=col(12), scale=col(11))
             act(v("oto", 960, 1024), v("W3", 1280, 1344), F.Identity, bias=col(12), scale=col(11))
             ot = (T.ot[:], [("ot", 1)])
-            dma("y", ot, (T.oto[1:128:16, :], v("oto")[1]), 32768)
-            for r in (2, 3):
-                dma("g", ot, (T.oto[r:128:16, :], v("oto")[1]), 200000, accum_op=A.add)
+            dma("y", ot, (T.oto[1:128:16, :], v("oto")[1]), 100000)
+            dma("g", ot, (T.oto[3:128:16, :], v("oto")[1]), 700000, accum_op=A.add)
         for b in range(4):
             mm(bank(4 + b, 128), quad("eq", b, 128), quad("es", b, 128), v("lq%d" % t), v("ls%d" % t),
-               ext=("ac%d" % t, 32, sent, FAR[0] + (3.0 if t == 0 else 0.0)))
+               ext=("ac%d" % t, 32, sent, FAR[0][t]))
             act(quad("Cw", b, 128), bank(4 + b, 128))
             act(v("Dw", 384 * b + C, 384 * b + 384), by(quad("Cw", b, 128), (T["ll%d" % t][:, 0:4], [])),
                 ext=("al%d" % t, 16, told, FAR[1]))

@@ -1,12 +1,21 @@
+import math
+import numpy as np
 from concourse.bass import DstId, RemoteDMATransfer
 from concourse.mybir import dt, AluOpType as A, ActivationFunctionType as F
 
 C, R = 320, 3
+FC, FK = 9, 11
 B16, F32, U16, I32, X4, U8 = "bfloat16", "float32", "uint16", "int32", "float8_e4m3fn_x4", "uint8"
-SHARE = {"G1": 16, "G2": 14, "G3": 30}
+SHARE = {"G1": (("s", 0, 20), ("s", 20, 40), ("v", 40, 60)),
+         "G2": (("s", 0, 20), ("s", 20, 40), ("v", 40, 60)),
+         "G3": (("s", 0, 18), ("s", 18, 36), ("v", 36, 64))}
 RUNS = ((0, 192), (192, C))
-CYC, FIXED, GATHER, SAME, OTHER, LOCAL, FAR = 0.001, 0.03, 1.7, 0.1, 0.2, 2.0, ((9.5, 9.0, 9.0), 6.5)
-TRIES, SHAKE = 3000, 30
+RUNS0, RUNS1 = ((0, C),), ((0, C),)
+PACE = ((0.00102, 1.56, (7.0, 5.0, 5.0), 3.8, 0.01, 0.08, 0.17), (0.00090, 1.3, (8.5, 6.0, 6.0), 4.8, 0.02, 0.06, 0.12),
+        (0.00120, 1.9, (7.0, 5.0, 5.0), 4.0, 0.02, 0.08, 0.15), (0.00100, 1.6, (7.0, 5.0, 5.0), 4.0, 0.0, 0.12, 0.25))
+LOCAL = 2.0
+PASSES, EASE, EARLY = 20, 0.15, 0.2
+TRIES = 90000
 SCRATCH = {"ps": ("psum", [128, 4096], F32)}
 PART = {}
 PLAN = {}
@@ -14,7 +23,7 @@ PLAN = {}
 
 def _sb(names, n, d):
     for s in names.split():
-        SCRATCH[s] = ("sbuf", [128, n], d)
+        SCRATCH[s] = ("sbuf", [128] + (n if isinstance(n, list) else [n]), d)
 
 
 def _parts(buf, names, n, d):
@@ -31,20 +40,22 @@ _sb("cq0 cq1 cq2 lq0 lq1 lq2", 128, X4); _sb("cs0 cs1 cs2 ls0 ls1 ls2", 128, U8)
 _sb("rq0 rq1 rq2", 64, X4); _sb("rs0 rs1 rs2", 64, U8)
 _sb("sl0 sl1 sl2 ll0 ll1 ll2", 4, U16); _sb("rl0 rl1 rl2", 2, U16)
 _sb("twi qi", 64, I32); _sb("pi", 4, I32); _sb("pf", 18, F32)
-_sb("Dw", 1536, B16); _sb("sw", 384, B16); _sb("U C2w TB3", 1024, B16); _sb("F3w", 1040, B16); _sb("W3", 1360, B16)
-_sb("G1w TB1 G2w TB2", 960, B16); _sb("TBs", C, B16); _sb("Gl TBl", 256, B16); _sb("Zw TBz", 128, B16)
-_sb("oto", 1024, F32); _sb("yb", C, F32)
-_sb("A0", 68, B16); _sb("offO offT offM", 64, U16); _sb("offL", 56, U16)
-_parts("fa", "A1 A2 Tp vb hc K sc dZO dN dY n1 n2 ys lo t1 t2 t3 t4 t5 t6 t7 t8 t9 sm fl", 64, F32)
-_parts("ba", "Ak kc dPk dZk b1 b2 b3 b4", 64, B16); _sb("goX", 100, B16); _sb("yy", 100, F32)
-for _n, _d in (("U0b", B16), ("U0c", B16), ("U0f", F32), ("U0g", F32)):
-    SCRATCH[_n] = ("sbuf", [128, 2, 2, 16], _d)
+_sb("Dw", 1536, B16); _sb("sw", 384, B16); _sb("C2w", 1168, B16); _sb("F3w W3", 1040, B16)
+_sb("G1w G2w", 960, B16); _sb("Gl", 256, B16); _sb("Zw", 128, B16)
+_sb("U", 1024, B16); _sb("TB", [32, 2, 16], B16); _sb("TB1 TB2", [30, 2, 16], B16); _sb("TBs", [10, 2, 16], B16); _sb("TBl TBz", [4, 2, 16], B16)
+_sb("AA", [32, 2, 2], B16); _sb("mid2", [2, 2, 2, 16], B16); _sb("mid1", [2, 2, 16], F32)
+_sb("GO", 320, B16); _sb("PA", 240, B16); _sb("PB", 120, B16); _sb("PC TQ PD PK KA KB", 128, F32)
+_sb("zz d1 lm", [4, 2], F32); _sb("fc", [5, 2, 2, 2], F32)
+_sb("oto", 1024, F32); _sb("yb", C, F32); _sb("beta", 128, F32)
+_sb("offO offT offM", 64, U16); _sb("offL", 56, U16)
+_parts("fa", "A1 A2 sc lo ys t1 t2 t3 t4 t5 t6 t8 t9 sm fl", 64, F32)
+_parts("ba", "kc b1", 64, B16); _sb("yy", 100, F32)
 SEMAPHORES = (["cv", "cs", "cp", "cg", "loc"] + ["d%d" % i for i in range(18)]
               + ["%s%d" % (s, t) for s in ("ac", "al", "rc", "rl") for t in range(R)])
 
 
 def _bits(es):
-    return sum(1 << e for e in es)
+    return sum(1 << int(e) for e in es)
 
 
 def _way(cores, r, side, topo):
@@ -66,6 +77,10 @@ def _engines(cores, r, topo):
     return out
 
 
+def _share(es, t, i):
+    return es if t else es[4 * i:4 * i + 4]
+
+
 def _to(topo, dst, src):
     rid, pid = topo.addr(dst, src)
     return [DstId(rid=rid, pnc=pid)]
@@ -75,16 +90,16 @@ def relay_program(g, core, T, topo, side, dst):
     es = topo.engines(core, dst)[:8]
     lo = 64 - 64 * side
     for t in range(R):
-        g.wait_ge(T.sem["rc%d" % t], 16)
-        for a, b in ((T["rq%d" % t][:, 0:64].bitcast(dt.uint8), T["lq%d" % t][:, lo:lo + 64].bitcast(dt.uint8)),
-                     (T["rs%d" % t][:, 0:64], T["ls%d" % t][:, lo:lo + 64])):
-            g.remote_dma_fused([RemoteDMATransfer(dst_ids=_to(topo, dst, core), dma_engine_mask=_bits(es),
+        g.wait_ge(T.sem["rc%d" % t], 2 * len(_share(es, t, 0)))
+        for i, a, b in ((0, T["rq%d" % t][:, 0:64].bitcast(dt.uint8), T["lq%d" % t][:, lo:lo + 64].bitcast(dt.uint8)),
+                        (1, T["rs%d" % t][:, 0:64], T["ls%d" % t][:, lo:lo + 64])):
+            g.remote_dma_fused([RemoteDMATransfer(dst_ids=_to(topo, dst, core), dma_engine_mask=_bits(_share(es, t, i)),
                                                   remote_sem=T.sem["ac%d" % t], src=a, dst=b)], local_sem=T.sem.loc)
         g.wait_ge(T.sem["rl%d" % t], 8)
         g.remote_dma_fused([RemoteDMATransfer(dst_ids=_to(topo, dst, core), dma_engine_mask=_bits(es), remote_sem=T.sem["al%d" % t],
                                               src=T["rl%d" % t][:, 0:2], dst=T["ll%d" % t][:, 2 - 2 * side:4 - 2 * side])],
                            local_sem=T.sem.loc)
-    g.wait_ge(T.sem.loc, 24 * R)
+    g.wait_ge(T.sem.loc, sum(8 + 2 * len(_share(es, t, 0)) for t in range(R)))
 
 
 def _order(ops):
@@ -95,37 +110,105 @@ def _order(ops):
             for m2, w2, j in seen.get(n, []):
                 if m & m2 and (w or w2 or (n == "ps" and ops[j]["q"] != o["q"])):
                     deps[j] = 1
-        o["deps"] = sorted(deps)
-        o["lag"] = [(j, ops[j]["late"] + (SAME if ops[j]["q"] == o["q"] else OTHER)) for j in o["deps"]] + o["after"]
+        o["all"] = 0
+        for j in deps:
+            o["all"] |= ops[j]["all"]
+        o["deps"] = [j for j in sorted(deps) if not o["all"] >> j & 1]
+        o["all"] |= _bits(deps)
         for n, m, w in o["acc"]:
             seen.setdefault(n, []).append((m, w, i))
     if "best" not in PLAN:
         n = len(ops)
-        cost, que = [o["cost"] for o in ops], [o["q"] for o in ops]
-        ahead = [o["lag"] for o in ops]
+        que = [o["q"] for o in ops]
+        late = [o["late"] for o in ops]
+        costs = [[o["cost"][s] for o in ops] for s in range(len(PACE))]
+        aheads = [[[(j, late[j] + PACE[s][5 if que[j] == o["q"] else 6]) for j in o["deps"]] + [(j, lag[s]) for j, lag in o["after"]]
+                   for o in ops] for s in range(len(PACE))]
+        cost, ahead = costs[0], aheads[0]
         behind = [[] for o in ops]
-        rank = [o["cost"] + o["late"] for o in ops]
+        rank = [cost[i] + late[i] for i in range(n)]
         for i in range(n - 1, -1, -1):
             for j, lag in ahead[i]:
                 rank[j] = max(rank[j], rank[i] + cost[j] + lag)
                 behind[j].append((i, lag))
-        seed, best = 1, None
-        for trial in range(TRIES):
+        best = None
+        for trial in range(PASSES):
             at = _place(cost, que, ahead, behind, rank, [0.0] * n)
-            end = max(at[i] + cost[i] + ops[i]["late"] for i in range(n))
-            if best is None or end <= best[0]:
-                best = (end, at)
-            at = list(best[1])
-            for k in range(SHAKE):
-                seed = (seed * 1103515245 + 12345) % 2147483648
-                at[(seed >> 8) % n] += ((seed >> 3) % 32 - 15.5) / 16.0
-            back = _place(cost, que, behind, ahead, [at[i] + cost[i] for i in range(n)], [o["late"] for o in ops])
+            order = sorted(range(n), key=lambda i: (at[i], i))
+            end = sum(_replay(order, 0, None, costs[s], que, aheads[s], late)[0] for s in range(len(PACE)))
+            if best is None or end < best[0]:
+                best = (end, order)
+            back = _place(cost, que, behind, ahead, [at[i] + cost[i] for i in range(n)], late)
             rank = [back[i] + cost[i] for i in range(n)]
+        above = [0] * n
+        for i in range(n):
+            for j, lag in ahead[i]:
+                above[i] |= above[j] | 1 << j
+        best = _polish(best[1], costs, que, aheads, late, above)
         PLAN["best"] = best
-    at = PLAN["best"][1]
-    for i, o in enumerate(ops):
-        o["at"] = at[i]
-    return sorted(range(len(ops)), key=lambda i: (at[i], i))
+    for k, i in enumerate(PLAN["best"][1]):
+        ops[i]["at"] = k
+    return PLAN["best"][1]
+
+
+def _replay(order, start, was, cost, que, ahead, late):
+    done, why = (list(was[2]), list(was[3])) if was else ([0.0] * len(order), [None] * len(order))
+    prev = {}
+    for i in order[max(0, start - 150):start]:
+        prev[que[i]] = i
+    for i in order[start:]:
+        w = prev.get(que[i])
+        t = 0.0 if w is None else done[w]
+        for j, lag in ahead[i]:
+            if done[j] + lag >= t:
+                t, w = done[j] + lag, j
+        why[i] = w
+        done[i] = t + cost[i]
+        prev[que[i]] = i
+    end, last = max((done[i] + late[i], i) for i in range(len(order)) if late[i])
+    return end + EARLY * sum(done) / len(done), last, done, why
+
+
+def _polish(order, costs, que, aheads, late, above):
+    n, seed = len(order), [1]
+
+    def draw(k):
+        seed[0] = (seed[0] * 1103515245 + 12345) % 2147483648
+        return (seed[0] >> 8) % k
+
+    now = [_replay(order, 0, None, costs[s], que, aheads[s], late) for s in range(len(PACE))]
+    best = (sum(c[0] for c in now), order)
+    for trial in range(TRIES):
+        end, i, done, why = now[draw(len(PACE))]
+        chain = draw(10) >= 3
+        i = i if chain else draw(n)
+        held = []
+        while why[i] is not None:
+            if que[why[i]] == que[i] and not above[i] >> why[i] & 1:
+                held.append((why[i], i))
+            i = why[i] if chain else order[0]
+        if not held:
+            continue
+        u, w = held[draw(len(held))]
+        a, b, k = order.index(u), order.index(w), (0, 0, 1, 2, 4, 8)[draw(6)]
+        if draw(2):
+            while k and a > 0:
+                a -= 1
+                k -= que[order[a]] == que[w]
+            ahead = [i for i in order[a:b + 1] if i == w or above[w] >> i & 1]
+        else:
+            while k and b < n - 1:
+                b += 1
+                k -= que[order[b]] == que[u]
+            ahead = [i for i in order[a:b + 1] if i != u and not above[i] >> u & 1]
+        new = order[:a] + ahead + [i for i in order[a:b + 1] if i not in ahead] + order[b + 1:]
+        then = [_replay(new, a, now[s], costs[s], que, aheads[s], late) for s in range(len(PACE))]
+        worse = sum(c[0] for c in then) - sum(c[0] for c in now)
+        if worse <= -EASE * (1.0 - trial / TRIES) ** 2 * math.log((draw(4096) + 1) / 4097.0):
+            order, now = new, then
+            if sum(c[0] for c in now) < best[0]:
+                best = (sum(c[0] for c in now), order)
+    return [_replay(best[1], 0, None, costs[s], que, aheads[s], late)[0] for s in range(len(PACE))], best[1]
 
 
 def _place(cost, que, ahead, behind, rank, first):
@@ -164,6 +247,7 @@ def rank_program(g, core, T, topo):
         return
     queue = {"v": g.vector, "s": g.scalar, "p": g.tensor, "g": g, "y": g.sync}
     ops = []
+    ALL, BOTH = slice(None), slice(FC, FK + 1, FK - FC)
 
     def v(name, lo=0, hi=None, step=1):
         name, base, n = PART.get(name, (name, 0, SCRATCH.get(name, [0, [0, 0]])[1][1]))
@@ -171,6 +255,11 @@ def rank_program(g, core, T, topo):
         cols = range(lo, hi, step)
         return (T[name][:, lo:hi:step] if step > 1 else T[name][:, lo:hi],
                 [(name, 1 << (lo // 512) if name == "ps" else _bits(cols))], len(cols), SCRATCH[name][2] in (B16, U16))
+
+    def nd(name, *idx):
+        shape = SCRATCH[name][1][1:]
+        cols = np.arange(int(np.prod(shape))).reshape(shape)[idx].reshape(-1)
+        return T[name][(ALL,) + idx], [(name, _bits(cols))], len(cols), SCRATCH[name][2] in (B16, U16)
 
     def by(win, off): return (win[0].indirect(off[0]), win[1] + off[1], 0, False)
     def raw(x): return (x[0].bitcast(dt.uint8), x[1], 4 * x[2], False)
@@ -182,67 +271,83 @@ def rank_program(g, core, T, topo):
             if isinstance(a, tuple):
                 acc += [(n, m, i < nout) for n, m in a[1]]
         ops.append({"q": q, "fn": fn, "args": [a[0] if isinstance(a, tuple) else a for a in args], "acc": acc, "kind": kind,
-                    "kw": {k: (kw[k][0] if isinstance(kw[k], tuple) else kw[k]) for k in kw}, "cost": cost, "late": late,
+                    "kw": {k: (kw[k][0] if isinstance(kw[k], tuple) else kw[k]) for k in kw}, "late": late,
+                    "cost": cost if isinstance(cost, list) else [cost] * len(PACE),
                     "ext": ext[:2] if ext else None, "after": [ext[2:]] if ext else []})
         return len(ops) - 1
 
     def price(o, a, x=1.0):
-        return FIXED + (0.05 + o[2] * GATHER * CYC if a[2] == 0 else max(64, o[2] * x) * CYC)
+        return [0.06 + o[2] * p[1] * p[0] if a[2] == 0 else p[4] + max(64, o[2] * x) * p[0] for p in PACE]
 
     def tt(o, a, b, op): call("v", g.vector.tensor_tensor, 1, [o, a, b, op], price(o, a, 1.0 if a[1][0][0] == "ps" else 2.0))
     def ts(o, a, s1, op0, s2=None, op1=None):
         call("v", g.vector.tensor_scalar, 1, [o, a, s1, s2, op0] + ([] if op1 is None else [op1]), price(o, a))
     def cp(o, a): call("v", g.vector.tensor_copy, 1, [o, a], price(o, a, 0.5 if o[3] and a[3] else 1.0))
     def tr(o, a): call("v", g.vector.transpose, 1, [o, a], price(o, a, 0.5 if o[3] else 1.0))
+    def scan(o, a, b, op0=A.mult, op1=A.add):
+        call("v", g.vector.tensor_tensor_scan, 1, [o, a, b, 0.0, op0, op1], price(o, a, 0.5 if o[3] and a[3] and b[3] else 1.0))
     def fill(o, x): call("v", g.vector.memset, 1, [o, x], price(o, o, 0.5))
-    def quant(o, s, a): call("v", g.vector.quantize_mx, 2, [o, s, a], FIXED + 0.012 + 0.27 * CYC * a[2])
+    def quant(o, s, a): call("v", g.vector.quantize_mx, 2, [o, s, a], [(15 + 0.27 * a[2]) * p[0] for p in PACE])
     def act(o, a, f=F.Copy, ext=None, **kw): call("s", g.scalar.activation, 1, [o, a, f], price(o, a), kw, ext=ext)
     def mm(o, w, ws, x, xs, ext=None):
         call("p", g.tensor.matmul_mx, 1, [o, w, ws, x, xs, True, True], (o[2] + 16) * 0.0006, ext=ext)
     def dma(q, o, a, nbytes, reads=(), **kw):
         call(q, queue[q].dma_start, 1, [o, a], 0.1, kw, kind="d", late=LOCAL + nbytes / 2e5, reads=reads)
     def iota(o, pat, base, cm=0, flt=True):
-        call("g", g.iota, 1, [o, pat, base, cm], 0.13 + 2 * o[2] * CYC, {"allow_small_or_imprecise_dtypes": True} if flt else {})
-    def fb(name, r, lo=0, hi=64): return v(name, r + 16 * lo, 16 * hi, 16)
+        call("g", g.iota, 1, [o, pat, base, cm], 0.13 + 2 * o[2] * 0.001, {"allow_small_or_imprecise_dtypes": True} if flt else {})
+    def fb(name, r, lo=0, hi=64): return nd(name, slice(lo // 2, hi // 2), ALL, r)
+    def st(name, k, n, lo=0, hi=60): return v(name, n * lo + k, n * hi, n)
+    def blk(name, lo, hi): return nd(name, slice(lo, hi))
+    def fa(r, lo=0, hi=64): return nd("AA", slice(lo // 2, hi // 2), ALL, r)
     def bank(i, n): return v("ps", 512 * i, 512 * i + n)
     def col(i): return v("pf", i, i + 1)
     def halves(name): return [v(name, e, 64, 2) for e in (0, 1)]
-    def fields(name, r): return [v(name, 16 * e + r, 1024, 32) for e in (0, 1)]
     def quad(name, b, n): return v(name, n * b, n * b + n)
 
-    def swap(u0, ins, outs):
+    def swap1(ins, outs):
         for e in (0, 1):
-            tr((T[u0][:, e], [(u0, _bits(range(32 * e, 32 * e + 32)))], 32, False), ins[e])
+            tr(nd("mid1", e), ins[e])
         for h in (0, 1):
-            tr(outs[h], (T[u0][:, :, h, :], [(u0, _bits(range(64)))], 32, False))
+            tr(outs[h], nd("mid1", ALL, h, ALL))
 
-    def turn(out, wide, t):
-        if t:
-            tr(v(out, 0, 960), v(wide, 0, 960))
-        else:
+    def swap2(ins, outs):
+        for e in (0, 1):
+            tr(nd("mid2", ALL, ALL, e, ALL), ins[e])
+        for h in (0, 1):
+            tr(outs[h], nd("mid2", ALL, h, ALL, ALL))
+
+    def pair(name): return [nd(name, ALL, e, BOTH) for e in (0, 1)]
+    twins = [nd("AA", ALL, e, ALL) for e in (0, 1)]
+
+    def gather(name, out, wide, win, off, t, turn):
+        for q, lo, hi in SHARE[name]:
+            at = (lo + 20 * turn) % 60 if t else lo
+            (act if q == "s" else cp)(v(wide, 16 * at, 16 * (at + hi - lo)), by(win, v(off, lo, hi)))
+            if t:
+                tr(blk(out, at // 2, (at + hi - lo) // 2), v(wide, 16 * at, 16 * (at + hi - lo)))
+        if not t:
             for k in range(3):
-                tr(v(out, C * k, C * k + C), v(wide, k, 960, 3))
-
-    def gather(out, o0, win, off, n, nv):
-        act(v(out, o0 + 16 * nv, o0 + 16 * n), by(win, v(off, nv, n)))
-        cp(v(out, o0, o0 + 16 * nv), by(win, v(off, 0, nv)))
+                tr(blk(out, 10 * ((k + turn) % 3), 10 * ((k + turn) % 3) + 10), v(wide, k, 960, 3))
 
     def double(lo, src, k):
         for h in (0, 1):
-            act(v("fl", lo + h, lo + 8, 2), src, F.Identity, scale=col(2 + h), bias=col(4 + 2 * k + h))
+            act(v("fl", lo + h, lo + 8, 2), src, F.Identity, scale=col(2 + h), bias=col(k + h))
 
     ways = [_way(cores, rank, s, topo) for s in (0, 1)]
     eng = _engines(cores, rank, topo)
 
-    def send(pieces, sems, reads):
+    def send(pieces, sems, reads, after, share):
         trs = []
         for side in (0, 1):
             stop, dst = ways[side]
-            n = 8 // len(pieces[side])
-            for i, (a, br, bd) in enumerate(pieces[side]):
-                trs.append(RemoteDMATransfer(dst_ids=_to(topo, stop, core), dma_engine_mask=_bits(eng[side][n * i:n * i + n]),
-                                             remote_sem=T.sem[sems[0] if stop == dst else sems[1]], src=a, dst=bd if stop == dst else br))
-        return call("g", g.remote_dma_fused, 0, [trs], 0.3, {"local_sem": T.sem.loc}, kind="r", reads=reads)
+            a, br, bd = pieces[side]
+            trs.append(RemoteDMATransfer(dst_ids=_to(topo, stop, core), dma_engine_mask=_bits(share(eng[side])),
+                                         remote_sem=T.sem[sems[0] if stop == dst else sems[1]], src=a, dst=bd if stop == dst else br))
+        i = call("g", g.remote_dma_fused, 0, [trs], 0.3, {"local_sem": T.sem.loc}, kind="r", reads=reads)
+        ops[i]["left"] = 2 * len(share(eng[0]))
+        if after is not None:
+            ops[i]["after"].append((after, [0.0] * len(PACE)))
+        return i
 
     dma("s", v("twi"), T.tw[:], 32768)
     dma("y", v("X0", 0, 1280), T.x[:], 327680)
@@ -255,180 +360,186 @@ def rank_program(g, core, T, topo):
     call("g", g.affine_select, 1, [v("em"), v("one"), [[-1, 528]], A.is_equal, 0.0, 3, 4], 1.25)
     for b in range(4):
         quant(quad("eq", b, 128), quad("es", b, 128), v("em", 3 - b, 515 - b))
-    fill(v("U"), 0.0)
+    fill(nd("TB", ALL), 0.0)
+    iota(v("U"), [[0, 1024]], 0)
     fill(v("sw", C, 384), 0.0)
-    fill(v("W3", 1344, 1360), 0.0)
+    fill(v("W3", 1024, 1040), 0.0)
     fill(v("F3w", 1024, 1040), 0.0)
+    fill(v("C2w", 960, 1024), 0.0)
+    fill(v("C2w", 1024, 1040), 1.0)
+    iota(v("beta"), [[1, 128]], 0)
+    act(v("C2w", 1040, 1168), v("beta"), F.Identity, scale=1.0 / 32)
     ts(v("pi", 1, 2), v("pi", 0, 1), 31, A.bitwise_and)
     ts(v("pi", 2, 3), v("pi", 0, 1), 15, A.bitwise_and)
     cp(v("pf", 0, 2), v("pi", 1, 3))
     ts(col(2), col(0), 16.0, A.is_lt)
     ts(col(3), col(0), 16.0, A.is_ge)
-    ts(col(13), col(1), 1.0, A.is_equal, 2.0, A.mult)
+    ts(col(13), col(1), float(FC), A.is_equal, 2.0, A.mult)
     ts(col(12), col(13), 288.0, A.mult)
     ts(col(11), col(13), 1.0, A.add)
-    for k, real, zero in ((0, 192.0, 1344.0), (1, 832.0, 960.0), (2, 192.0, 960.0), (6, -1.0, 1024.0)):
-        ts(v("pf", 4 + 2 * k, 6 + 2 * k), v("pf", 2, 4), real - zero, A.mult, zero, A.add)
+    for k, real, zero in ((4, 32.0, 1024.0), (6, -1.0, 1024.0), (8, 192.0, 0.0)):
+        ts(v("pf", k, k + 2), v("pf", 2, 4), real - zero, A.mult, zero, A.add)
     iota(v("t8", 0, 60), [[0, 3], [32, 10], [0, 2]], -192)
     iota(v("kc", 0, 60), [[C, 3], [0, 20]], 0)
     iota(v("sm", 32, 36), [[32, 2], [0, 2]], 128)
-    iota(v("sm", 36, 40), [[-64, 2], [16, 2]], 64)
-    iota(v("dPk", 0, 20), [[0, 20]], 2 * C)
-    iota(v("dPk", 20, 60), [[0, 40]], -C)
+    iota(v("sm", 36, 40), [[-64, 2], [16, 2]], 1040 + 64)
     for t in range(R):
         iota(v("X%d" % t, 1280, 1536), [[0, 256]], 0)
-    ts(v("vb", 0, 60), v("t8", 0, 60), col(0), A.add)
+    ts(st("PA", 2, 4), v("t8", 0, 60), col(0), A.add)
+    act(st("PA", 1, 4), st("PA", 2, 4), F.Identity, scale=-1.0)
+    fill(st("PA", 3, 4), 0.0)
+    fill(st("GO", 0, 4, 0, 80), 0.0)
+    fill(st("GO", 1, 2, 0, 160), 1.0)
+    fill(st("KA", 0, 2), -1e9)
     ts(v("sm", 16, 20), v("sm", 36, 40), col(1), A.add)
-    ts(v("t9", 0, 60), v("vb", 0, 60), -960.0, A.mult, 143360.0, A.add)
-    tt(v("hc", 0, 60), v("t9", 0, 60), v("kc", 0, 60), A.subtract)
+    for h in (0, 1):
+        ts(nd("d1", ALL, h), v("sm", 16, 20), col(3 - h), A.mult, col(8 + h), A.add)
+    ts(v("t9", 0, 60), st("PA", 2, 4), -960.0, A.mult, 143360.0, A.add)
+    tt(st("KB", 1, 2), v("t9", 0, 60), v("kc", 0, 60), A.subtract)
     quant(v("uq"), v("us"), v("ub"))
     quant(v("vq"), v("vs"), v("vb_"))
     cp(v("A2"), v("twi"))
-    ts(v("t1"), v("A2"), -577.0, A.add, 1.0 / 3.0, A.mult)
-    ts(v("t2"), v("A2"), -832.0, A.add)
-    ts(v("t3"), v("A2"), 960.0, A.is_ge, 640.0, A.mult)
+    ts(v("t1"), v("twi"), -577.0, A.add, 1.0 / 3.0, A.mult)
+    act(v("t2"), v("A2"), F.Identity, bias=-832.0)
+    ts(v("t3"), v("twi"), 960.0, A.is_ge, 640.0, A.mult)
     cp(v("qi"), v("t1"))
-    ts(v("t4"), v("A2"), -576.0, A.add, 320.0, A.mult)
+    act(v("t4"), v("A2"), F.Identity, scale=320.0, bias=-576.0 * 320.0)
     ts(v("t5"), v("qi"), -960.0, A.mult)
-    tt(v("A0", 0, 64), v("qi"), v("t2"), A.max)
+    tt(fa(0), v("qi"), v("t2"), A.max)
     tt(v("t6"), v("t4"), v("t5"), A.add)
-    ts(v("offO"), v("A0", 0, 64), 192.0, A.add)
-    tt(v("Ak"), v("t6"), v("t3"), A.max)
-    swap("U0b", halves("A0"), fields("U", 1))
-    swap("U0c", halves("Ak"), fields("U", 2))
-    tt(v("A1"), v("A0", 0, 64), v("Ak"), A.add)
-    tr(v("F3w", 0, 1024), v("U"))
-    turn("TB3", "F3w", 0)
-    tr(v("TB3", 960, 1024), v("F3w", 960, 1024))
-    ts(fb("U", 1, 60, 64), v("sm", 32, 36), col(0), A.add)
-    fill(fb("U", 2, 60, 64), 640.0)
-    ts(fb("U", 3, 60, 64), fb("U", 1, 60, 64), -2.0, A.mult, 256.0, A.add)
-    tt(v("Tp"), fb("TB3", 1), fb("TB3", 2), A.add)
+    ts(v("offO", 0, 60), fa(0, 0, 60), 192.0, A.add)
+    tt(fa(1), v("t6"), v("t3"), A.max)
+    swap2(twins, pair("TB"))
+    tr(v("F3w", 0, 1024), nd("TB", ALL))
+    for k in range(3):
+        tr(blk("TB", 10 * k, 10 * k + 10), v("F3w", k, 960, 3))
+    tr(blk("TB", 30, 32), v("F3w", 960, 1024))
+    act(st("U", FC, 16, 60, 64), v("sm", 32, 36), F.Identity, bias=col(0))
+    fill(st("U", FK, 16, 60, 64), 640.0)
     quant(v("q0"), v("s0"), v("X0", 0, 1280))
 
     for t in range(R):
+        unit = 1.0 if t == R - 1 else float(C)
         for lo, hi in (RUNS if t else ((0, C),)):
             mm(bank(4, hi - lo), v("uq"), v("us"), v("q%d" % t, lo, hi), v("s%d" % t, lo, hi))
             act(v("sw", lo, hi), bank(4, hi - lo), F.Sign, bias=-1e-36)
         for b in range(4):
             mm(bank(b, C), quad("eq", b, 128), quad("es", b, 128), v("q%d" % t), v("s%d" % t))
             act(v("Dw", 384 * b, 384 * b + C), bank(b, C))
-        ts(v("offT"), v("A1"), 192.0, A.add)
+        tt(st("PC", 1, 2, 0, 64), fb("TB", FC), fb("TB", FK), A.add)
+        tt(v("A1", 0, 60), fa(0, 0, 60), fa(1, 0, 60), A.add)
+        ts(v("offT", 0, 60), v("A1", 0, 60), 192.0, A.add)
+        act(v("sm", 0, 4), fa(1, 60, 64), F.Abs, bias=-800.0, scale=2.0)
+        tt(v("sm", 4, 8), v("sm", 0, 4), fa(0, 60, 64), A.add)
+        double(0, v("sm", 4, 8), 4)
         if t:
-            double(0, v("A1", 60, 64), 0)
+            cp(v("offL", 0, 8), v("fl", 0, 8))
+            act(v("Zw"), by(v("W3"), v("offL", 0, 8)))
         else:
-            ts(v("sm", 48, 52), v("Ak", 60, 64), 0.0, A.is_equal, 3.0, A.mult)
+            ts(v("sm", 48, 52), fa(1, 60, 64), 0.0, A.is_equal, 3.0, A.mult)
             tt(v("sm", 52, 56), v("sm", 48, 52), v("A2", 60, 64), A.add)
-            double(0, v("sm", 52, 56), 6)
-        ts(v("sm", 0, 4), v("A1", 60, 64), 128.0, A.is_ge, -960.0, A.mult)
-        tt(v("sm", 4, 8), v("sm", 0, 4), v("A1", 60, 64), A.add)
-        double(8, v("sm", 4, 8), 1)
-        cp(v("offL", 0, 8), v("fl", 0, 8))
-        act(v("Zw"), by(v("W3" if t else "F3w"), v("offL", 0, 8)))
-        tr(v("TBz"), v("Zw"))
-        tt(v("A0", 64, 68), v("TBz", 1, 128, 32), v("TBz", 17, 128, 32), A.add)
-        tt(v("sm", 8, 12), v("TBz", 2, 128, 32), v("TBz", 18, 128, 32), A.add)
-        tt(v("sm", 12, 16), v("sm", 8, 12), v("A0", 64, 68), A.add)
-        double(16, v("sm", 12, 16), 2)
-        for r in (1, 2):
-            act(fb("U", 3 + r, 0, 40), fb("TB3", r, 20, 60))
-            act(fb("U", 3 + r, 40, 60), fb("TB3", r, 0, 20))
-        act(v("n1", 0, 60), fb("TB3", 1, 0, 60), F.Identity, bias=143360.0, scale=-960.0)
-        tt(v("t3", 0, 60), v("n1", 0, 60), fb("TB3", 2, 0, 60), A.subtract)
-        tt(v("K", 0, 60), v("t3", 0, 60), v("hc", 0, 60), A.max)
-        act(v("b1", 0, 60), fb("TB3", 2, 0, 60), F.Abs, bias=-800.0, scale=2.0)
+            double(8, v("sm", 52, 56), 6)
+            cp(v("offL", 0, 16), v("fl", 0, 16))
+            act(v("Zw"), by(v("F3w"), v("offL", 8, 16)))
+        tr(nd("TBz", ALL), v("Zw"))
+        tt(nd("zz", ALL), nd("TBz", ALL, 0, BOTH), nd("TBz", ALL, 1, BOTH), A.add)
+        tt(v("sm", 12, 16), nd("zz", ALL, 0), nd("zz", ALL, 1), A.add)
+        for h in (0, 1):
+            act(nd("lm", ALL, h), v("sm", 12, 16), F.Identity, scale=col(2 + h))
+        tt(nd("fc", 0), nd("lm", ALL), nd("d1", ALL), A.add)
+        act(st("KB", 0, 2), fb("TB", FC, 0, 60), F.Identity, bias=143360.0, scale=-960.0)
+        act(st("KA", 1, 2), fb("TB", FK, 0, 60), F.Identity, scale=-1.0)
+        scan(v("PK", 0, 120), v("KA", 0, 120), v("KB", 0, 120), A.add, A.max)
+        act(v("b1", 0, 60), fb("TB", FK, 0, 60), F.Abs, bias=-2.5 * unit, scale=2.0 * unit / C)
         for c in range(3):
-            act(quad("dZk", c, 20), quad("b1", (c + 2) % 3, 20), F.Identity, bias=-160.0 - C * c)
-        act(v("n2", 20, 60), fb("TB3", 1, 0, 40))
-        act(v("n2", 0, 20), fb("TB3", 1, 40, 60))
-        tt(v("dZO", 0, 60), v("n2", 0, 60), v("vb", 0, 60), A.subtract)
-        act(v("t2", 0, 40), v("Tp", 20, 60))
-        act(v("t2", 40, 60), v("Tp", 0, 20))
-        tt(v("dN", 0, 60), v("t2", 0, 60), v("Tp", 0, 60), A.subtract)
+            act(st("PB", 0, 2, 20 * c, 20 * c + 20), quad("b1", (c + 2) % 3, 20), F.Identity, bias=-unit * (c + 0.5))
+        act(st("PA", 0, 4, 20, 60), fb("TB", FC, 0, 40))
+        act(st("PA", 0, 4, 0, 20), fb("TB", FC, 40, 60))
+        act(v("t2", 0, 40), st("PC", 1, 2, 20, 60))
+        act(v("t2", 40, 60), st("PC", 1, 2, 0, 20))
+        tt(st("PC", 0, 2), v("t2", 0, 60), st("PC", 1, 2), A.subtract)
+        act(st("TQ", 1, 2, 60, 64), st("PC", 1, 2, 60, 64))
+        if t == R - 1:
+            act(st("U", FK, 16, 60, 64), st("U", FC, 16, 60, 64), F.Identity, scale=-2.0, bias=256.0)
         for b in range(4):
-            act(v("fl", 24 + 8 * b, 32 + 8 * b), v("A0", 60, 68), F.Identity, scale=4.0, bias=768.0 + b)
-        cp(v("offL", 24, 56), v("fl", 24, 56))
-        cp(v("offL", 8, 24), v("fl", 8, 24))
+            for c, src in ((0, fa(0, 60, 64)), (1, nd("zz", ALL, 0))):
+                act(nd("fc", 1 + b, ALL, c, ALL), src, F.Identity, scale=4.0, bias=768.0 + b)
+        if t:
+            cp(v("offL", 16, 56), nd("fc", ALL))
+        else:
+            cp(v("offL", 24, 56), nd("fc", slice(1, 5)))
+            cp(v("offL", 16, 24), nd("fc", 0))
         for b in range(4):
             act(v("ct%d" % t, b, 512, 4), by(v("X%d" % t), quad("offL", 3 + b, 8)))
         quant(v("cq%d" % t), v("cs%d" % t), v("ct%d" % t))
-        for src, rel, land, f in (("cq", "rq", "lq", lambda a: a.bitcast(dt.uint8)), ("cs", "rs", "ls", lambda a: a)):
-            sent = send([[(f(T["%s%d" % (src, t)][:, 32 * side + 64 * i:32 * side + 64 * i + 32]),
-                           f(T["%s%d" % (rel, t)][:, 32 * i:32 * i + 32]),
-                           f(T["%s%d" % (land, t)][:, 64 - 64 * side + 32 * i:96 - 64 * side + 32 * i])) for i in (0, 1)]
-                         for side in (0, 1)], ("ac%d" % t, "rc%d" % t), [v("%s%d" % (src, t))])
-        gather("G1w", 0, v("sw"), "offO", 60, SHARE["G1"])
-        tr(v("TBs"), v("sw", 0, C))
+        sent = None
+        for i, src, rel, land, f in ((0, "cq", "rq", "lq", lambda a: a.bitcast(dt.uint8)), (1, "cs", "rs", "ls", lambda a: a)):
+            sent = send([(f(T["%s%d" % (src, t)][:, 64 * side:64 * side + 64]), f(T["%s%d" % (rel, t)][:, 0:64]),
+                          f(T["%s%d" % (land, t)][:, 64 - 64 * side:128 - 64 * side])) for side in (0, 1)],
+                        ("ac%d" % t, "rc%d" % t), [v("%s%d" % (src, t))], sent, lambda es: _share(es, t, i))
+        gather("G1", "TB1", "G1w", v("sw"), "offO", t, 1)
+        tr(nd("TBs", ALL), v("sw", 0, C))
         for k in range(3):
-            tt(quad("sc", k, 20), fb("TBs", t, 0, 20), quad("K", k, 20), A.mult)
-        turn("TB1", "G1w", t)
+            tt(quad("sc", (k + 1) % 3, 20), fb("TBs", t, 0, 20), st("PK", 1, 2, 20 * k, 20 * k + 20), A.mult)
         tt(v("yy", 0, 60), fb("TB1", t, 0, 60), v("sc", 0, 60), A.mult)
         tt(v("yy", 60, 100), fb("TB1", t, 0, 40), v("sc", 0, 40), A.mult)
         tt(v("lo", 0, 60), v("yy", 20, 80), v("yy", 40, 100), A.min)
         ts(v("t9", 0, 60), v("lo", 0, 60), -1.0, A.min)
-        tt(fb("U", 0, 0, 60), v("yy", 0, 60), v("t9", 0, 60), A.is_lt)
-        tr(v("C2w"), v("U"))
+        tt(fb("TB", 0, 0, 60), v("yy", 0, 60), v("t9", 0, 60), A.is_lt)
+        tr(v("C2w", 0, 640), blk("TB", 10, 30))
+        tr(v("C2w", 640, 960), blk("TB", 0, 10))
         act(v("Gl", 128, 256), by(v("C2w"), v("offL", 16, 24)), F.Identity, scale=32.0)
-        cp(v("Gl", 0, 128), by(v("C2w"), v("offL", 8, 16)))
-        tr(v("TBl"), v("Gl"))
-        tt(v("sm", 24, 32), v("TBl", 0, 256, 32), v("TBl", 16, 256, 32), A.add)
-        for c in range(4):
-            ts(v("sl%d" % t, c, c + 1), v("sm", 24 + c, 25 + c), v("sm", 28 + c, 29 + c), A.mult, v("sm", 16 + c, 17 + c), A.add)
-        told = send([[(T["sl%d" % t][:, 2 * side:2 * side + 2], T["rl%d" % t][:, 0:2], T["ll%d" % t][:, 2 - 2 * side:4 - 2 * side])]
-                     for side in (0, 1)], ("al%d" % t, "rl%d" % t), [v("sl%d" % t)])
-        ops[told]["after"].append((sent, 0.0))
-        gather("G2w", 0, v("C2w"), "offT", 60, SHARE["G2"])
-        turn("TB2", "G2w", t)
-        tt(v("goX", 20, 80), fb("TB2", 0, 0, 60), fb("U", 0, 0, 60), A.mult)
-        tt(v("goX", 0, 20), fb("TB2", 0, 40, 60), fb("U", 0, 40, 60), A.mult)
-        tt(v("goX", 80, 100), fb("TB2", 0, 0, 20), fb("U", 0, 0, 20), A.mult)
-        tt(v("ys", 0, 40), fb("TB2", 4, 20, 60), fb("TB2", 5, 20, 60), A.add)
-        tt(v("ys", 40, 60), fb("TB2", 4, 0, 20), fb("TB2", 5, 0, 20), A.add)
-        tt(v("dY", 0, 60), v("ys", 0, 60), v("Tp", 0, 60), A.subtract)
-        gp, gn = v("goX", 0, 60), v("goX", 40, 100)
-        tt(v("t1", 0, 60), gp, v("dZO", 0, 60), A.mult)
-        tt(v("b2", 0, 60), gn, v("dPk", 0, 60), A.mult)
-        tt(v("b3", 0, 60), gp, v("dZk", 0, 60), A.mult)
-        tt(v("t4", 0, 60), gp, v("dN", 0, 60), A.mult)
-        tt(v("t5", 0, 60), gn, v("dY", 0, 60), A.mult)
-        tt(fb("U", 1, 0, 60), v("t1", 0, 60), v("vb", 0, 60), A.add)
-        tt(v("b4", 0, 60), v("b2", 0, 60), v("kc", 0, 60), A.add)
-        tt(v("t7", 0, 60), v("t4", 0, 60), v("Tp", 0, 60), A.add)
-        tt(fb("U", 2, 0, 60), v("b4", 0, 60), v("b3", 0, 60), A.add)
-        tt(v("Tp", 0, 60), v("t7", 0, 60), v("t5", 0, 60), A.add)
-        if t == R - 1:
-            ts(fb("U", 3, 0, 60), fb("U", 2, 0, 60), 1.0 / C, A.mult)
+        tt(v("Gl", 0, 128), by(v("C2w"), v("offL", 0, 8)), v("Gl", 128, 256), A.mult)
+        tr(nd("TBl", ALL), v("Gl", 0, 128))
+        tt(v("sm", 24, 28), nd("TBl", ALL, 0, 0), nd("TBl", ALL, 1, 0), A.add)
+        cp(v("sl%d" % t), v("sm", 24, 28))
+        told = send([(T["sl%d" % t][:, 2 * side:2 * side + 2], T["rl%d" % t][:, 0:2], T["ll%d" % t][:, 2 - 2 * side:4 - 2 * side])
+                     for side in (0, 1)], ("al%d" % t, "rl%d" % t), [v("sl%d" % t)], sent, lambda es: es)
+        gather("G2", "TB2", "G2w", v("C2w", 0, 1024), "offT", t, 1)
+        tt(st("GO", 2, 4, 20, 80), fb("TB2", 0, 0, 60), fb("TB", 0, 0, 60), A.mult)
+        tt(st("GO", 2, 4, 0, 20), fb("TB2", 0, 40, 60), fb("TB", 0, 40, 60), A.mult)
+        tt(v("ys", 0, 20), fb("TB2", FC, 40, 60), fb("TB2", FK, 40, 60), A.add)
+        tt(v("ys", 20, 60), fb("TB2", FC, 0, 40), fb("TB2", FK, 0, 40), A.add)
+        gp, gn = v("GO", 80, 320, 2), v("GO", 0, 240, 2)
+        for c in range(3):
+            act(st("PB", 1, 2, 20 * c, 20 * c + 20), st("GO", 2, 4, 20 * c, 20 * c + 20), F.Identity,
+                scale=unit * (-1.0 if c else 2.0), bias=unit * c)
+        scan(v("U", FC - 8, 960, 4), v("GO", 80, 320), v("PA"))
+        scan(v("U", FK - 8, 960, 8), gp, v("PB"))
+        scan(v("PD", 0, 120), gp, v("PC", 0, 120))
+        tt(st("PD", 0, 2), v("ys", 0, 60), st("PC", 1, 2), A.subtract)
+        scan(v("TQ", 0, 120), gn, v("PD", 0, 120))
         tr(v("F3w", 0, 1024), v("U"))
-        swap("U0f", halves("Tp"), halves("A2"))
+        swap1([v("TQ", 1 + 2 * e, 128, 4) for e in (0, 1)], halves("A2"))
         ts(v("offM"), v("A2"), 192.0, A.add)
-        gather("W3", C, v("F3w", 0, 1024), "offM", 64, SHARE["G3"])
-        tr(v("TB3"), v("W3", C, 1344))
-        swap("U0b", fields("TB3", 1), halves("A0"))
-        ts(v("offO"), v("A0", 0, 64), 192.0, A.add)
-        if t < R - 1:
-            act(v("W3", 0, C), v("W3", 960, 1280))
-            tt(v("Tp"), fb("TB3", 1), fb("TB3", 2), A.add)
-            swap("U0g", halves("Tp"), halves("A1"))
-        else:
+        gather("G3", "TB", "W3", v("F3w", 0, 1024), "offM", 1, 0)
+        swap2(pair("TB"), twins)
+        ts(v("offO", 0, 60), fa(0, 0, 60), 192.0, A.add)
+        if t == R - 1:
             for k in range(3):
-                act(v("oto", k, 960, 3), v("W3", C + C * k, 640 + C * k), F.Identity, bias=col(12), scale=col(11))
-            act(v("oto", 960, 1024), v("W3", 1280, 1344), F.Identity, bias=col(12), scale=col(11))
+                act(v("oto", k, 960, 3), v("W3", C * k, C + C * k), F.Identity, bias=col(12), scale=col(11))
+            act(v("oto", 960, 1024), v("W3", 960, 1024), F.Identity, bias=col(12), scale=col(11))
             ot = (T.ot[:], [("ot", 1)])
-            dma("y", ot, (T.oto[1:128:16, :], v("oto")[1]), 100000)
-            dma("g", ot, (T.oto[3:128:16, :], v("oto")[1]), 700000, accum_op=A.add)
+            dma("y", ot, (T.oto[FC:128:16, :], v("oto")[1]), 100000)
+            dma("g", ot, (T.oto[FK:128:16, :], v("oto")[1]), 700000, accum_op=A.add)
         for b in range(4):
             mm(bank(4 + b, 128), quad("eq", b, 128), quad("es", b, 128), v("lq%d" % t), v("ls%d" % t),
-               ext=("ac%d" % t, 32, sent, FAR[0][t]))
+               ext=("ac%d" % t, 4 * len(_share(eng[0], t, 0)), sent, [p[2][t] for p in PACE]))
             act(quad("Cw", b, 128), bank(4 + b, 128))
             act(v("Dw", 384 * b + C, 384 * b + 384), by(quad("Cw", b, 128), (T["ll%d" % t][:, 0:4], [])),
-                ext=("al%d" % t, 16, told, FAR[1]))
-        for lo, hi in RUNS:
-            n, a, z = hi - lo, lo // 16, hi // 16
+                ext=("al%d" % t, 16, told, [p[3] for p in PACE]))
+        for lo, hi in RUNS0:
             for b in range(4):
-                win, p0, tm = quad("Dw", b, 384), v("p0", C * b + lo, C * b + hi), v("tm", C * b + lo, C * b + hi)
-                act(p0, by(win, v("offO", a, z)))
-                tt(tm, by(win, v("offO", 20 + a, 20 + z)), p0, A.max)
-                tt(v("M%d" % t, 4 * lo + b, 4 * hi, 4), by(win, v("offO", 40 + a, 40 + z)), tm, A.max)
+                act(v("p0", C * b + lo, C * b + hi), by(quad("Dw", b, 384), v("offO", lo // 16, hi // 16)))
+        for lo, hi in RUNS1:
+            for b in range(4):
+                tt(v("tm", C * b + lo, C * b + hi), by(quad("Dw", b, 384), v("offO", 20 + lo // 16, 20 + hi // 16)),
+                   v("p0", C * b + lo, C * b + hi), A.max)
+        for lo, hi in RUNS:
+            n = hi - lo
+            for b in range(4):
+                tt(v("M%d" % t, 4 * lo + b, 4 * hi, 4), by(quad("Dw", b, 384), v("offO", 40 + lo // 16, 40 + hi // 16)),
+                   v("tm", C * b + lo, C * b + hi), A.max)
             mq, ms = v("mq%d" % t, lo, hi), v("ms%d" % t, lo, hi)
             quant(mq, ms, v("M%d" % t, 4 * lo, 4 * hi))
             for b in range(4):
@@ -466,7 +577,7 @@ def rank_program(g, core, T, topo):
             wait(q, o["ext"][0], o["ext"][1], {})
         ins = o["fn"](*o["args"], **o["kw"])
         if o["kind"] == "r":
-            nsent += 16
+            nsent += o["left"]
             continue
         sem, inc = ("c" + q, 1) if o["kind"] == "c" else ("d%d" % ndma, 16)
         ndma += o["kind"] == "d"

@@ -8,11 +8,11 @@ FC, FK = 9, 11
 B16, F32, U16, I32, X4, U8 = "bfloat16", "float32", "uint16", "int32", "float8_e4m3fn_x4", "uint8"
 SHARE = {"G1": (("s", 0, 20), ("s", 20, 40), ("v", 40, 60)),
          "G2": (("s", 0, 20), ("s", 20, 40), ("v", 40, 60)),
-         "G3": (("s", 0, 18), ("s", 18, 36), ("v", 36, 64))}
+         "G3": (("s", 0, 34), ("v", 34, 64)),
+         "G10": (("s", 0, 44), ("v", 44, 60)), "G20": (("s", 0, 34), ("v", 34, 60))}
 RUNS = ((0, 192), (192, C))
-RUNS0, RUNS1 = ((0, C),), ((0, C),)
-PACE = ((0.00102, 1.56, (7.0, 5.0, 5.0), 3.8, 0.01, 0.08, 0.17), (0.00090, 1.3, (8.5, 6.0, 6.0), 4.8, 0.02, 0.06, 0.12),
-        (0.00120, 1.9, (7.0, 5.0, 5.0), 4.0, 0.02, 0.08, 0.15), (0.00100, 1.6, (7.0, 5.0, 5.0), 4.0, 0.0, 0.12, 0.25))
+PACE = ((0.00102, 1.56, (6.2, 5.0, 5.0), 3.8, 0.01, 0.08, 0.17), (0.00090, 1.3, (7.0, 5.5, 5.5), 4.4, 0.02, 0.06, 0.12),
+        (0.00120, 1.9, (6.5, 5.0, 5.0), 4.0, 0.02, 0.08, 0.15), (0.00100, 1.6, (6.2, 5.0, 5.0), 4.0, 0.0, 0.12, 0.25))
 LOCAL = 2.0
 PASSES, EASE, EARLY = 20, 0.15, 0.2
 TRIES = 90000
@@ -50,7 +50,7 @@ _sb("oto", 1024, F32); _sb("yb", C, F32); _sb("beta", 128, F32)
 _sb("offO offT offM", 64, U16); _sb("offL", 56, U16)
 _parts("fa", "A1 A2 sc lo ys t1 t2 t3 t4 t5 t6 t8 t9 sm fl", 64, F32)
 _parts("ba", "kc b1", 64, B16); _sb("yy", 100, F32)
-SEMAPHORES = (["cv", "cs", "cp", "cg", "loc"] + ["d%d" % i for i in range(18)]
+SEMAPHORES = (["cv", "cs", "cp", "cg", "loc"] + ["d%d" % i for i in range(19)]
               + ["%s%d" % (s, t) for s in ("ac", "al", "rc", "rl") for t in range(R)])
 
 
@@ -289,6 +289,7 @@ def rank_program(g, core, T, topo):
     def fill(o, x): call("v", g.vector.memset, 1, [o, x], price(o, o, 0.5))
     def quant(o, s, a): call("v", g.vector.quantize_mx, 2, [o, s, a], [(15 + 0.27 * a[2]) * p[0] for p in PACE])
     def act(o, a, f=F.Copy, ext=None, **kw): call("s", g.scalar.activation, 1, [o, a, f], price(o, a), kw, ext=ext)
+    def put(o, x): act(o, v("one", 0, o[2]), F.Identity, scale=x)
     def mm(o, w, ws, x, xs, ext=None):
         call("p", g.tensor.matmul_mx, 1, [o, w, ws, x, xs, True, True], (o[2] + 16) * 0.0006, ext=ext)
     def dma(q, o, a, nbytes, reads=(), **kw):
@@ -320,7 +321,7 @@ def rank_program(g, core, T, topo):
     twins = [nd("AA", ALL, e, ALL) for e in (0, 1)]
 
     def gather(name, out, wide, win, off, t, turn):
-        for q, lo, hi in SHARE[name]:
+        for q, lo, hi in SHARE[name if t else name + "0"]:
             at = (lo + 20 * turn) % 60 if t else lo
             (act if q == "s" else cp)(v(wide, 16 * at, 16 * (at + hi - lo)), by(win, v(off, lo, hi)))
             if t:
@@ -350,8 +351,9 @@ def rank_program(g, core, T, topo):
         return i
 
     dma("s", v("twi"), T.tw[:], 32768)
-    dma("y", v("X0", 0, 1280), T.x[:], 327680)
-    dma("s", v("ub"), T.u[:], 131072)
+    dma("y", v("X0", 0, 768), T.x[:, 0:768], 230000)
+    dma("s", v("ub"), T.u[:], 360000)
+    dma("y", v("X0", 768, 1280), T.x[:, 768:1280], 490000)
     dma("y", raw(v("wq")), T.wc[:], 262144, [v("X0", 0, 1280)])
     dma("y", v("wsb"), T.ws[:], 65536, [v("X0", 0, 1280)])
     dma("y", v("vb_"), T.v[:], 131072, [v("X0", 0, 1280)])
@@ -360,13 +362,14 @@ def rank_program(g, core, T, topo):
     call("g", g.affine_select, 1, [v("em"), v("one"), [[-1, 528]], A.is_equal, 0.0, 3, 4], 1.25)
     for b in range(4):
         quant(quad("eq", b, 128), quad("es", b, 128), v("em", 3 - b, 515 - b))
+    made = range(len(ops) - 4, len(ops) - 1)
     fill(nd("TB", ALL), 0.0)
     iota(v("U"), [[0, 1024]], 0)
-    fill(v("sw", C, 384), 0.0)
-    fill(v("W3", 1024, 1040), 0.0)
-    fill(v("F3w", 1024, 1040), 0.0)
-    fill(v("C2w", 960, 1024), 0.0)
-    fill(v("C2w", 1024, 1040), 1.0)
+    put(v("sw", C, 384), 0.0)
+    put(v("W3", 1024, 1040), 0.0)
+    put(v("F3w", 1024, 1040), 0.0)
+    put(v("C2w", 960, 1024), 0.0)
+    put(v("C2w", 1024, 1040), 1.0)
     iota(v("beta"), [[1, 128]], 0)
     act(v("C2w", 1040, 1168), v("beta"), F.Identity, scale=1.0 / 32)
     ts(v("pi", 1, 2), v("pi", 0, 1), 31, A.bitwise_and)
@@ -375,34 +378,34 @@ def rank_program(g, core, T, topo):
     ts(col(2), col(0), 16.0, A.is_lt)
     ts(col(3), col(0), 16.0, A.is_ge)
     ts(col(13), col(1), float(FC), A.is_equal, 2.0, A.mult)
-    ts(col(12), col(13), 288.0, A.mult)
-    ts(col(11), col(13), 1.0, A.add)
+    act(col(12), col(13), F.Identity, scale=288.0)
+    act(col(11), col(13), F.Identity, bias=1.0)
     for k, real, zero in ((4, 32.0, 1024.0), (6, -1.0, 1024.0), (8, 192.0, 0.0)):
-        ts(v("pf", k, k + 2), v("pf", 2, 4), real - zero, A.mult, zero, A.add)
+        act(v("pf", k, k + 2), v("pf", 2, 4), F.Identity, scale=real - zero, bias=zero)
     iota(v("t8", 0, 60), [[0, 3], [32, 10], [0, 2]], -192)
     iota(v("kc", 0, 60), [[C, 3], [0, 20]], 0)
     iota(v("sm", 32, 36), [[32, 2], [0, 2]], 128)
     iota(v("sm", 36, 40), [[-64, 2], [16, 2]], 1040 + 64)
     for t in range(R):
         iota(v("X%d" % t, 1280, 1536), [[0, 256]], 0)
-    ts(st("PA", 2, 4), v("t8", 0, 60), col(0), A.add)
+    act(st("PA", 2, 4), v("t8", 0, 60), F.Identity, bias=col(0))
     act(st("PA", 1, 4), st("PA", 2, 4), F.Identity, scale=-1.0)
-    fill(st("PA", 3, 4), 0.0)
-    fill(st("GO", 0, 4, 0, 80), 0.0)
-    fill(st("GO", 1, 2, 0, 160), 1.0)
-    fill(st("KA", 0, 2), -1e9)
-    ts(v("sm", 16, 20), v("sm", 36, 40), col(1), A.add)
+    put(st("PA", 3, 4), 0.0)
+    put(st("GO", 0, 4, 0, 80), 0.0)
+    put(st("GO", 1, 2, 0, 160), 1.0)
+    put(st("KA", 0, 2), -1e9)
+    act(v("sm", 16, 20), v("sm", 36, 40), F.Identity, bias=col(1))
     for h in (0, 1):
-        ts(nd("d1", ALL, h), v("sm", 16, 20), col(3 - h), A.mult, col(8 + h), A.add)
-    ts(v("t9", 0, 60), st("PA", 2, 4), -960.0, A.mult, 143360.0, A.add)
+        act(nd("d1", ALL, h), v("sm", 16, 20), F.Identity, scale=col(3 - h), bias=col(8 + h))
+    act(v("t9", 0, 60), st("PA", 2, 4), F.Identity, scale=-960.0, bias=143360.0)
     tt(st("KB", 1, 2), v("t9", 0, 60), v("kc", 0, 60), A.subtract)
     quant(v("uq"), v("us"), v("ub"))
     quant(v("vq"), v("vs"), v("vb_"))
     cp(v("A2"), v("twi"))
-    ts(v("t1"), v("twi"), -577.0, A.add, 1.0 / 3.0, A.mult)
+    ops[-1]["after"] += [(j, [0.0] * len(PACE)) for j in made]
+    ts(v("qi"), v("twi"), -577.0, A.add, 1.0 / 3.0, A.mult)
     act(v("t2"), v("A2"), F.Identity, bias=-832.0)
     ts(v("t3"), v("twi"), 960.0, A.is_ge, 640.0, A.mult)
-    cp(v("qi"), v("t1"))
     act(v("t4"), v("A2"), F.Identity, scale=320.0, bias=-576.0 * 320.0)
     ts(v("t5"), v("qi"), -960.0, A.mult)
     tt(fa(0), v("qi"), v("t2"), A.max)
@@ -415,14 +418,15 @@ def rank_program(g, core, T, topo):
         tr(blk("TB", 10 * k, 10 * k + 10), v("F3w", k, 960, 3))
     tr(blk("TB", 30, 32), v("F3w", 960, 1024))
     act(st("U", FC, 16, 60, 64), v("sm", 32, 36), F.Identity, bias=col(0))
-    fill(st("U", FK, 16, 60, 64), 640.0)
-    quant(v("q0"), v("s0"), v("X0", 0, 1280))
+    put(st("U", FK, 16, 60, 64), 640.0)
+    for lo, hi in RUNS:
+        quant(v("q0", lo, hi), v("s0", lo, hi), v("X0", 4 * lo, 4 * hi))
 
     for t in range(R):
         unit = 1.0 if t == R - 1 else float(C)
-        for lo, hi in (RUNS if t else ((0, C),)):
-            mm(bank(4, hi - lo), v("uq"), v("us"), v("q%d" % t, lo, hi), v("s%d" % t, lo, hi))
-            act(v("sw", lo, hi), bank(4, hi - lo), F.Sign, bias=-1e-36)
+        for i, (lo, hi) in enumerate(RUNS):
+            mm(bank(4 + i, hi - lo), v("uq"), v("us"), v("q%d" % t, lo, hi), v("s%d" % t, lo, hi))
+            act(v("sw", lo, hi), bank(4 + i, hi - lo), F.Sign, bias=-1e-36)
         for b in range(4):
             mm(bank(b, C), quad("eq", b, 128), quad("es", b, 128), v("q%d" % t), v("s%d" % t))
             act(v("Dw", 384 * b, 384 * b + C), bank(b, C))
@@ -509,7 +513,9 @@ def rank_program(g, core, T, topo):
         scan(v("PD", 0, 120), gp, v("PC", 0, 120))
         tt(st("PD", 0, 2), v("ys", 0, 60), st("PC", 1, 2), A.subtract)
         scan(v("TQ", 0, 120), gn, v("PD", 0, 120))
-        tr(v("F3w", 0, 1024), v("U"))
+        if t != 1:
+            tr(v("F3w", 960, 1024), v("U", 960, 1024))
+        tr(v("F3w", 0, 960), v("U", 0, 960))
         swap1([v("TQ", 1 + 2 * e, 128, 4) for e in (0, 1)], halves("A2"))
         ts(v("offM"), v("A2"), 192.0, A.add)
         gather("G3", "TB", "W3", v("F3w", 0, 1024), "offM", 1, 0)
@@ -521,20 +527,17 @@ def rank_program(g, core, T, topo):
             act(v("oto", 960, 1024), v("W3", 960, 1024), F.Identity, bias=col(12), scale=col(11))
             ot = (T.ot[:], [("ot", 1)])
             dma("y", ot, (T.oto[FC:128:16, :], v("oto")[1]), 100000)
-            dma("g", ot, (T.oto[FK:128:16, :], v("oto")[1]), 700000, accum_op=A.add)
+            dma("g", ot, (T.oto[FK:128:16, :], v("oto")[1]), 450000, accum_op=A.add)
         for b in range(4):
             mm(bank(4 + b, 128), quad("eq", b, 128), quad("es", b, 128), v("lq%d" % t), v("ls%d" % t),
                ext=("ac%d" % t, 4 * len(_share(eng[0], t, 0)), sent, [p[2][t] for p in PACE]))
             act(quad("Cw", b, 128), bank(4 + b, 128))
             act(v("Dw", 384 * b + C, 384 * b + 384), by(quad("Cw", b, 128), (T["ll%d" % t][:, 0:4], [])),
                 ext=("al%d" % t, 16, told, [p[3] for p in PACE]))
-        for lo, hi in RUNS0:
-            for b in range(4):
-                act(v("p0", C * b + lo, C * b + hi), by(quad("Dw", b, 384), v("offO", lo // 16, hi // 16)))
-        for lo, hi in RUNS1:
-            for b in range(4):
-                tt(v("tm", C * b + lo, C * b + hi), by(quad("Dw", b, 384), v("offO", 20 + lo // 16, 20 + hi // 16)),
-                   v("p0", C * b + lo, C * b + hi), A.max)
+        for b in range(4):
+            for lo, hi in (((0, C),) if b or t < R - 1 else RUNS):
+                (cp if lo else act)(v("p0", C * b + lo, C * b + hi), by(quad("Dw", b, 384), v("offO", lo // 16, hi // 16)))
+            tt(quad("tm", b, C), by(quad("Dw", b, 384), v("offO", 20, 40)), quad("p0", b, C), A.max)
         for lo, hi in RUNS:
             n = hi - lo
             for b in range(4):
@@ -549,11 +552,12 @@ def rank_program(g, core, T, topo):
                 tt(v("X%d" % (t + 1), 4 * lo + b, 4 * hi, 4), v("ps", 512 * b + lo, 512 * b + hi), rr, A.add)
             q, s = v("q%d" % (t + 1), lo, hi), v("s%d" % (t + 1), lo, hi)
             quant(q, s, v("X%d" % (t + 1), 4 * lo, 4 * hi))
-            if t == R - 1:
-                mm(bank(4, n), v("vq"), v("vs"), q, s)
-                (cp if hi == C else act)(v("yb", lo, hi), bank(4, n))
-                dma("s" if hi == C else "y", T.y[:, lo:hi], v("yb", lo, hi), 512 * n)
-                dma("y", T.oc[:, 4 * lo:4 * hi], raw(q), 512 * n)
+    for i, (lo, hi) in enumerate(RUNS):
+        n, q, s = hi - lo, v("q%d" % R, lo, hi), v("s%d" % R, lo, hi)
+        mm(bank(4 + i, n), v("vq"), v("vs"), q, s)
+        act(v("yb", lo, hi), bank(4 + i, n))
+        dma("s" if i else "y", T.y[:, lo:hi], v("yb", lo, hi), 512 * n)
+        dma("y", T.oc[:, 4 * lo:4 * hi], raw(q), 512 * n)
     for k in range(4):
         dma("s" if k < 2 else "y", T.osc[4 * k:4 * k + 4, :], (T.s3[32 * k:32 * k + 4, :], v("s3")[1]), 1280)
 

import math
import numpy as np
from concourse.bass import DstId, RemoteDMATransfer
from concourse.mybir import dt, AluOpType as A, ActivationFunctionType as F

C, R = 320, 3
FC, FK = 9, 11
B16, F32, U16, I32, X4, U8 = "bfloat16", "float32", "uint16", "int32", "float8_e4m3fn_x4", "uint8"
SHARE = {"G1": (("s", 0, 20), ("s", 20, 40), ("v", 40, 60)),
         "G2": (("s", 0, 20), ("s", 20, 40), ("v", 40, 60)),
         "G3": (("s", 0, 34), ("v", 34, 64)),
         "G10": (("s", 0, 44), ("v", 44, 60)), "G20": (("s", 0, 34), ("v", 34, 60))}
RUNS = ((0, 192), (192, C))
PACE = ((0.00102, 1.56, (6.2, 5.0, 5.0), 3.8, 0.01, 0.08, 0.17), (0.00090, 1.3, (7.0, 5.5, 5.5), 4.4, 0.02, 0.06, 0.12),
        (0.00120, 1.9, (6.5, 5.0, 5.0), 4.0, 0.02, 0.08, 0.15), (0.00100, 1.6, (6.2, 5.0, 5.0), 4.0, 0.0, 0.12, 0.25))
LOCAL = 2.0
PASSES, EASE, EARLY = 20, 0.15, 0.2
TRIES = 90000
SCRATCH = {"ps": ("psum", [128, 4096], F32)}
PART = {}
PLAN = {}


def _sb(names, n, d):
    for s in names.split():
        SCRATCH[s] = ("sbuf", [128] + (n if isinstance(n, list) else [n]), d)


def _parts(buf, names, n, d):
    for i, s in enumerate(names.split()):
        PART[s] = (buf, n * i, n)
    _sb(buf, n * len(names.split()), d)


_sb("X0 X1 X2", 1536, B16); _sb("X3 M0 M1 M2 p0 tm", 1280, B16); _sb("rr", 1280, F32)
_sb("q0 q1 q2 q3 mq0 mq1 mq2", C, X4); _sb("s0 s1 s2 s3 ms0 ms1 ms2", C, U8)
_sb("ub vb_ ct0 ct1 ct2 Cw", 512, B16); _sb("uq vq", 128, X4); _sb("us vs", 128, U8)
_sb("wq eq", 512, X4); _sb("wsb es", 512, U8); _sb("one em", 528, B16)
_sb("cq0 cq1 cq2 lq0 lq1 lq2", 128, X4); _sb("cs0 cs1 cs2 ls0 ls1 ls2", 128, U8)
_sb("rq0 rq1 rq2", 64, X4); _sb("rs0 rs1 rs2", 64, U8)
_sb("sl0 sl1 sl2 ll0 ll1 ll2", 4, U16); _sb("rl0 rl1 rl2", 2, U16)
_sb("twi qi", 64, I32); _sb("pi", 4, I32); _sb("pf", 18, F32)
_sb("Dw", 1536, B16); _sb("sw", 384, B16); _sb("C2w", 1168, B16); _sb("F3w W3", 1040, B16)
_sb("G1w G2w", 960, B16); _sb("Gl", 256, B16); _sb("Zw", 128, B16)
_sb("U", 1024, B16); _sb("TB", [32, 2, 16], B16); _sb("TB1 TB2", [30, 2, 16], B16); _sb("TBs", [10, 2, 16], B16); _sb("TBl TBz", [4, 2, 16], B16)
_sb("AA", [32, 2, 2], B16); _sb("mid2", [2, 2, 2, 16], B16); _sb("mid1", [2, 2, 16], F32)
_sb("GO", 320, B16); _sb("PA", 240, B16); _sb("PB", 120, B16); _sb("PC TQ PD PK KA KB", 128, F32)
_sb("zz d1 lm", [4, 2], F32); _sb("fc", [5, 2, 2, 2], F32)
_sb("oto", 1024, F32); _sb("yb", C, F32); _sb("beta", 128, F32)
_sb("offO offT offM", 64, U16); _sb("offL", 56, U16)
_parts("fa", "A1 A2 sc lo ys t1 t2 t3 t4 t5 t6 t8 t9 sm fl", 64, F32)
_parts("ba", "kc b1", 64, B16); _sb("yy", 100, F32)
SEMAPHORES = (["cv", "cs", "cp", "cg", "loc"] + ["d%d" % i for i in range(19)]
              + ["%s%d" % (s, t) for s in ("ac", "al", "rc", "rl") for t in range(R)])


def _bits(es):
    return sum(1 << int(e) for e in es)


def _way(cores, r, side, topo):
    src, dst = cores[r], cores[(r + 1 - 2 * side) % len(cores)]
    if topo.may_write(src, dst):
        return dst, dst
    far = [c for c in topo.cores_of(src) if c != src and topo.may_write(c, dst)]
    far = [c for c in far if topo.die(c) == topo.die(src)] + [c for c in far if topo.die(c) != topo.die(src)]
    return far[side], dst


def _engines(cores, r, topo):
    src = cores[r]
    ch = [topo.engines(src, _way(cores, r, s, topo)[0]) for s in (0, 1)]
    first = 0 if len(ch[0]) <= len(ch[1]) else 1
    out = [None, None]
    out[first] = ch[first][:8]
    out[1 - first] = [e for e in ch[1 - first] if e not in out[first]][:8]
    return out


def _share(es, t, i):
    return es if t else es[4 * i:4 * i + 4]


def _to(topo, dst, src):
    rid, pid = topo.addr(dst, src)
    return [DstId(rid=rid, pnc=pid)]


def relay_program(g, core, T, topo, side, dst):
    es = topo.engines(core, dst)[:8]
    lo = 64 - 64 * side
    for t in range(R):
        g.wait_ge(T.sem["rc%d" % t], 2 * len(_share(es, t, 0)))
        for i, a, b in ((0, T["rq%d" % t][:, 0:64].bitcast(dt.uint8), T["lq%d" % t][:, lo:lo + 64].bitcast(dt.uint8)),
                        (1, T["rs%d" % t][:, 0:64], T["ls%d" % t][:, lo:lo + 64])):
            g.remote_dma_fused([RemoteDMATransfer(dst_ids=_to(topo, dst, core), dma_engine_mask=_bits(_share(es, t, i)),
                                                  remote_sem=T.sem["ac%d" % t], src=a, dst=b)], local_sem=T.sem.loc)
        g.wait_ge(T.sem["rl%d" % t], 8)
        g.remote_dma_fused([RemoteDMATransfer(dst_ids=_to(topo, dst, core), dma_engine_mask=_bits(es), remote_sem=T.sem["al%d" % t],
                                              src=T["rl%d" % t][:, 0:2], dst=T["ll%d" % t][:, 2 - 2 * side:4 - 2 * side])],
                           local_sem=T.sem.loc)
    g.wait_ge(T.sem.loc, sum(8 + 2 * len(_share(es, t, 0)) for t in range(R)))


def _order(ops):
    seen = {}
    for i, o in enumerate(ops):
        deps = {}
        for n, m, w in o["acc"]:
            for m2, w2, j in seen.get(n, []):
                if m & m2 and (w or w2 or (n == "ps" and ops[j]["q"] != o["q"])):
                    deps[j] = 1
        o["all"] = 0
        for j in deps:
            o["all"] |= ops[j]["all"]
        o["deps"] = [j for j in sorted(deps) if not o["all"] >> j & 1]
        o["all"] |= _bits(deps)
        for n, m, w in o["acc"]:
            seen.setdefault(n, []).append((m, w, i))
    if "best" not in PLAN:
        n = len(ops)
        que = [o["q"] for o in ops]
        late = [o["late"] for o in ops]
        costs = [[o["cost"][s] for o in ops] for s in range(len(PACE))]
        aheads = [[[(j, late[j] + PACE[s][5 if que[j] == o["q"] else 6]) for j in o["deps"]] + [(j, lag[s]) for j, lag in o["after"]]
                   for o in ops] for s in range(len(PACE))]
        cost, ahead = costs[0], aheads[0]
        behind = [[] for o in ops]
        rank = [cost[i] + late[i] for i in range(n)]
        for i in range(n - 1, -1, -1):
            for j, lag in ahead[i]:
                rank[j] = max(rank[j], rank[i] + cost[j] + lag)
                behind[j].append((i, lag))
        best = None
        for trial in range(PASSES):
            at = _place(cost, que, ahead, behind, rank, [0.0] * n)
            order = sorted(range(n), key=lambda i: (at[i], i))
            end = sum(_replay(order, 0, None, costs[s], que, aheads[s], late)[0] for s in range(len(PACE)))
            if best is None or end < best[0]:
                best = (end, order)
            back = _place(cost, que, behind, ahead, [at[i] + cost[i] for i in range(n)], late)
            rank = [back[i] + cost[i] for i in range(n)]
        above = [0] * n
        for i in range(n):
            for j, lag in ahead[i]:
                above[i] |= above[j] | 1 << j
        best = _polish(best[1], costs, que, aheads, late, above)
        PLAN["best"] = best
    for k, i in enumerate(PLAN["best"][1]):
        ops[i]["at"] = k
    return PLAN["best"][1]


def _replay(order, start, was, cost, que, ahead, late):
    done, why = (list(was[2]), list(was[3])) if was else ([0.0] * len(order), [None] * len(order))
    prev = {}
    for i in order[max(0, start - 150):start]:
        prev[que[i]] = i
    for i in order[start:]:
        w = prev.get(que[i])
        t = 0.0 if w is None else done[w]
        for j, lag in ahead[i]:
            if done[j] + lag >= t:
                t, w = done[j] + lag, j
        why[i] = w
        done[i] = t + cost[i]
        prev[que[i]] = i
    end, last = max((done[i] + late[i], i) for i in range(len(order)) if late[i])
    return end + EARLY * sum(done) / len(done), last, done, why


def _polish(order, costs, que, aheads, late, above):
    n, seed = len(order), [1]

    def draw(k):
        seed[0] = (seed[0] * 1103515245 + 12345) % 2147483648
        return (seed[0] >> 8) % k

    now = [_replay(order, 0, None, costs[s], que, aheads[s], late) for s in range(len(PACE))]
    best = (sum(c[0] for c in now), order)
    for trial in range(TRIES):
        end, i, done, why = now[draw(len(PACE))]
        chain = draw(10) >= 3
        i = i if chain else draw(n)
        held = []
        while why[i] is not None:
            if que[why[i]] == que[i] and not above[i] >> why[i] & 1:
                held.append((why[i], i))
            i = why[i] if chain else order[0]
        if not held:
            continue
        u, w = held[draw(len(held))]
        a, b, k = order.index(u), order.index(w), (0, 0, 1, 2, 4, 8)[draw(6)]
        if draw(2):
            while k and a > 0:
                a -= 1
                k -= que[order[a]] == que[w]
            ahead = [i for i in order[a:b + 1] if i == w or above[w] >> i & 1]
        else:
            while k and b < n - 1:
                b += 1
                k -= que[order[b]] == que[u]
            ahead = [i for i in order[a:b + 1] if i != u and not above[i] >> u & 1]
        new = order[:a] + ahead + [i for i in order[a:b + 1] if i not in ahead] + order[b + 1:]
        then = [_replay(new, a, now[s], costs[s], que, aheads[s], late) for s in range(len(PACE))]
        worse = sum(c[0] for c in then) - sum(c[0] for c in now)
        if worse <= -EASE * (1.0 - trial / TRIES) ** 2 * math.log((draw(4096) + 1) / 4097.0):
            order, now = new, then
            if sum(c[0] for c in now) < best[0]:
                best = (sum(c[0] for c in now), order)
    return [_replay(best[1], 0, None, costs[s], que, aheads[s], late)[0] for s in range(len(PACE))], best[1]


def _place(cost, que, ahead, behind, rank, first):
    left = [len(a) for a in ahead]
    ready = [i for i in range(len(cost)) if not left[i]]
    at, busy = [0.0] * len(cost), {}
    while ready:
        i = max(ready, key=lambda i: rank[i])
        ready.remove(i)
        t = max([first[i]] + [at[j] + cost[j] + lag for j, lag in ahead[i]])
        line = busy.setdefault(que[i], [])
        k = len(line)
        while k and line[k - 1][1] > t:
            k -= 1
        while k < len(line) and t + cost[i] > line[k][0] + 1e-9:
            t = max(t, line[k][1])
            k += 1
        line.insert(k, (t, t + cost[i]))
        at[i] = t
        for j, lag in behind[i]:
            left[j] -= 1
            if not left[j]:
                ready.append(j)
    return at


def rank_program(g, core, T, topo):
    cores = list(T.cores)
    rank = T.rank_of(core)
    if rank is None:
        for r in range(len(cores)):
            for side in (0, 1):
                stop, dst = _way(cores, r, side, topo)
                if stop == core:
                    relay_program(g, core, T, topo, side, dst)
        return
    queue = {"v": g.vector, "s": g.scalar, "p": g.tensor, "g": g, "y": g.sync}
    ops = []
    ALL, BOTH = slice(None), slice(FC, FK + 1, FK - FC)

    def v(name, lo=0, hi=None, step=1):
        name, base, n = PART.get(name, (name, 0, SCRATCH.get(name, [0, [0, 0]])[1][1]))
        lo, hi = base + lo, base + (n if hi is None else hi)
        cols = range(lo, hi, step)
        return (T[name][:, lo:hi:step] if step > 1 else T[name][:, lo:hi],
                [(name, 1 << (lo // 512) if name == "ps" else _bits(cols))], len(cols), SCRATCH[name][2] in (B16, U16))

    def nd(name, *idx):
        shape = SCRATCH[name][1][1:]
        cols = np.arange(int(np.prod(shape))).reshape(shape)[idx].reshape(-1)
        return T[name][(ALL,) + idx], [(name, _bits(cols))], len(cols), SCRATCH[name][2] in (B16, U16)

    def by(win, off): return (win[0].indirect(off[0]), win[1] + off[1], 0, False)
    def raw(x): return (x[0].bitcast(dt.uint8), x[1], 4 * x[2], False)

    def call(q, fn, nout, args, cost, kw=None, kind="c", ext=None, reads=(), late=0.0):
        kw = kw or {}
        acc = []
        for i, a in enumerate(list(args) + list(kw.values()) + list(reads)):
            if isinstance(a, tuple):
                acc += [(n, m, i < nout) for n, m in a[1]]
        ops.append({"q": q, "fn": fn, "args": [a[0] if isinstance(a, tuple) else a for a in args], "acc": acc, "kind": kind,
                    "kw": {k: (kw[k][0] if isinstance(kw[k], tuple) else kw[k]) for k in kw}, "late": late,
                    "cost": cost if isinstance(cost, list) else [cost] * len(PACE),
                    "ext": ext[:2] if ext else None, "after": [ext[2:]] if ext else []})
        return len(ops) - 1

    def price(o, a, x=1.0):
        return [0.06 + o[2] * p[1] * p[0] if a[2] == 0 else p[4] + max(64, o[2] * x) * p[0] for p in PACE]

    def tt(o, a, b, op): call("v", g.vector.tensor_tensor, 1, [o, a, b, op], price(o, a, 1.0 if a[1][0][0] == "ps" else 2.0))
    def ts(o, a, s1, op0, s2=None, op1=None):
        call("v", g.vector.tensor_scalar, 1, [o, a, s1, s2, op0] + ([] if op1 is None else [op1]), price(o, a))
    def cp(o, a): call("v", g.vector.tensor_copy, 1, [o, a], price(o, a, 0.5 if o[3] and a[3] else 1.0))
    def tr(o, a): call("v", g.vector.transpose, 1, [o, a], price(o, a, 0.5 if o[3] else 1.0))
    def scan(o, a, b, op0=A.mult, op1=A.add):
        call("v", g.vector.tensor_tensor_scan, 1, [o, a, b, 0.0, op0, op1], price(o, a, 0.5 if o[3] and a[3] and b[3] else 1.0))
    def fill(o, x): call("v", g.vector.memset, 1, [o, x], price(o, o, 0.5))
    def quant(o, s, a): call("v", g.vector.quantize_mx, 2, [o, s, a], [(15 + 0.27 * a[2]) * p[0] for p in PACE])
    def act(o, a, f=F.Copy, ext=None, **kw): call("s", g.scalar.activation, 1, [o, a, f], price(o, a), kw, ext=ext)
    def put(o, x): act(o, v("one", 0, o[2]), F.Identity, scale=x)
    def mm(o, w, ws, x, xs, ext=None):
        call("p", g.tensor.matmul_mx, 1, [o, w, ws, x, xs, True, True], (o[2] + 16) * 0.0006, ext=ext)
    def dma(q, o, a, nbytes, reads=(), **kw):
        call(q, queue[q].dma_start, 1, [o, a], 0.1, kw, kind="d", late=LOCAL + nbytes / 2e5, reads=reads)
    def iota(o, pat, base, cm=0, flt=True):
        call("g", g.iota, 1, [o, pat, base, cm], 0.13 + 2 * o[2] * 0.001, {"allow_small_or_imprecise_dtypes": True} if flt else {})
    def fb(name, r, lo=0, hi=64): return nd(name, slice(lo // 2, hi // 2), ALL, r)
    def st(name, k, n, lo=0, hi=60): return v(name, n * lo + k, n * hi, n)
    def blk(name, lo, hi): return nd(name, slice(lo, hi))
    def fa(r, lo=0, hi=64): return nd("AA", slice(lo // 2, hi // 2), ALL, r)
    def bank(i, n): return v("ps", 512 * i, 512 * i + n)
    def col(i): return v("pf", i, i + 1)
    def halves(name): return [v(name, e, 64, 2) for e in (0, 1)]
    def quad(name, b, n): return v(name, n * b, n * b + n)

    def swap1(ins, outs):
        for e in (0, 1):
            tr(nd("mid1", e), ins[e])
        for h in (0, 1):
            tr(outs[h], nd("mid1", ALL, h, ALL))

    def swap2(ins, outs):
        for e in (0, 1):
            tr(nd("mid2", ALL, ALL, e, ALL), ins[e])
        for h in (0, 1):
            tr(outs[h], nd("mid2", ALL, h, ALL, ALL))

    def pair(name): return [nd(name, ALL, e, BOTH) for e in (0, 1)]
    twins = [nd("AA", ALL, e, ALL) for e in (0, 1)]

    def gather(name, out, wide, win, off, t, turn):
        for q, lo, hi in SHARE[name if t else name + "0"]:
            at = (lo + 20 * turn) % 60 if t else lo
            (act if q == "s" else cp)(v(wide, 16 * at, 16 * (at + hi - lo)), by(win, v(off, lo, hi)))
            if t:
                tr(blk(out, at // 2, (at + hi - lo) // 2), v(wide, 16 * at, 16 * (at + hi - lo)))
        if not t:
            for k in range(3):
                tr(blk(out, 10 * ((k + turn) % 3), 10 * ((k + turn) % 3) + 10), v(wide, k, 960, 3))

    def double(lo, src, k):
        for h in (0, 1):
            act(v("fl", lo + h, lo + 8, 2), src, F.Identity, scale=col(2 + h), bias=col(k + h))

    ways = [_way(cores, rank, s, topo) for s in (0, 1)]
    eng = _engines(cores, rank, topo)

    def send(pieces, sems, reads, after, share):
        trs = []
        for side in (0, 1):
            stop, dst = ways[side]
            a, br, bd = pieces[side]
            trs.append(RemoteDMATransfer(dst_ids=_to(topo, stop, core), dma_engine_mask=_bits(share(eng[side])),
                                         remote_sem=T.sem[sems[0] if stop == dst else sems[1]], src=a, dst=bd if stop == dst else br))
        i = call("g", g.remote_dma_fused, 0, [trs], 0.3, {"local_sem": T.sem.loc}, kind="r", reads=reads)
        ops[i]["left"] = 2 * len(share(eng[0]))
        if after is not None:
            ops[i]["after"].append((after, [0.0] * len(PACE)))
        return i

    dma("s", v("twi"), T.tw[:], 32768)
    dma("y", v("X0", 0, 768), T.x[:, 0:768], 230000)
    dma("s", v("ub"), T.u[:], 360000)
    dma("y", v("X0", 768, 1280), T.x[:, 768:1280], 490000)
    dma("y", raw(v("wq")), T.wc[:], 262144, [v("X0", 0, 1280)])
    dma("y", v("wsb"), T.ws[:], 65536, [v("X0", 0, 1280)])
    dma("y", v("vb_"), T.v[:], 131072, [v("X0", 0, 1280)])
    iota(v("pi", 0, 1), [[0, 1]], 0, 1, False)
    fill(v("one"), 1.0)
    call("g", g.affine_select, 1, [v("em"), v("one"), [[-1, 528]], A.is_equal, 0.0, 3, 4], 1.25)
    for b in range(4):
        quant(quad("eq", b, 128), quad("es", b, 128), v("em", 3 - b, 515 - b))
    made = range(len(ops) - 4, len(ops) - 1)
    fill(nd("TB", ALL), 0.0)
    iota(v("U"), [[0, 1024]], 0)
    put(v("sw", C, 384), 0.0)
    put(v("W3", 1024, 1040), 0.0)
    put(v("F3w", 1024, 1040), 0.0)
    put(v("C2w", 960, 1024), 0.0)
    put(v("C2w", 1024, 1040), 1.0)
    iota(v("beta"), [[1, 128]], 0)
    act(v("C2w", 1040, 1168), v("beta"), F.Identity, scale=1.0 / 32)
    ts(v("pi", 1, 2), v("pi", 0, 1), 31, A.bitwise_and)
    ts(v("pi", 2, 3), v("pi", 0, 1), 15, A.bitwise_and)
    cp(v("pf", 0, 2), v("pi", 1, 3))
    ts(col(2), col(0), 16.0, A.is_lt)
    ts(col(3), col(0), 16.0, A.is_ge)
    ts(col(13), col(1), float(FC), A.is_equal, 2.0, A.mult)
    act(col(12), col(13), F.Identity, scale=288.0)
    act(col(11), col(13), F.Identity, bias=1.0)
    for k, real, zero in ((4, 32.0, 1024.0), (6, -1.0, 1024.0), (8, 192.0, 0.0)):
        act(v("pf", k, k + 2), v("pf", 2, 4), F.Identity, scale=real - zero, bias=zero)
    iota(v("t8", 0, 60), [[0, 3], [32, 10], [0, 2]], -192)
    iota(v("kc", 0, 60), [[C, 3], [0, 20]], 0)
    iota(v("sm", 32, 36), [[32, 2], [0, 2]], 128)
    iota(v("sm", 36, 40), [[-64, 2], [16, 2]], 1040 + 64)
    for t in range(R):
        iota(v("X%d" % t, 1280, 1536), [[0, 256]], 0)
    act(st("PA", 2, 4), v("t8", 0, 60), F.Identity, bias=col(0))
    act(st("PA", 1, 4), st("PA", 2, 4), F.Identity, scale=-1.0)
    put(st("PA", 3, 4), 0.0)
    put(st("GO", 0, 4, 0, 80), 0.0)
    put(st("GO", 1, 2, 0, 160), 1.0)
    put(st("KA", 0, 2), -1e9)
    act(v("sm", 16, 20), v("sm", 36, 40), F.Identity, bias=col(1))
    for h in (0, 1):
        act(nd("d1", ALL, h), v("sm", 16, 20), F.Identity, scale=col(3 - h), bias=col(8 + h))
    act(v("t9", 0, 60), st("PA", 2, 4), F.Identity, scale=-960.0, bias=143360.0)
    tt(st("KB", 1, 2), v("t9", 0, 60), v("kc", 0, 60), A.subtract)
    quant(v("uq"), v("us"), v("ub"))
    quant(v("vq"), v("vs"), v("vb_"))
    cp(v("A2"), v("twi"))
    ops[-1]["after"] += [(j, [0.0] * len(PACE)) for j in made]
    ts(v("qi"), v("twi"), -577.0, A.add, 1.0 / 3.0, A.mult)
    act(v("t2"), v("A2"), F.Identity, bias=-832.0)
    ts(v("t3"), v("twi"), 960.0, A.is_ge, 640.0, A.mult)
    act(v("t4"), v("A2"), F.Identity, scale=320.0, bias=-576.0 * 320.0)
    ts(v("t5"), v("qi"), -960.0, A.mult)
    tt(fa(0), v("qi"), v("t2"), A.max)
    tt(v("t6"), v("t4"), v("t5"), A.add)
    ts(v("offO", 0, 60), fa(0, 0, 60), 192.0, A.add)
    tt(fa(1), v("t6"), v("t3"), A.max)
    swap2(twins, pair("TB"))
    tr(v("F3w", 0, 1024), nd("TB", ALL))
    for k in range(3):
        tr(blk("TB", 10 * k, 10 * k + 10), v("F3w", k, 960, 3))
    tr(blk("TB", 30, 32), v("F3w", 960, 1024))
    act(st("U", FC, 16, 60, 64), v("sm", 32, 36), F.Identity, bias=col(0))
    put(st("U", FK, 16, 60, 64), 640.0)
    for lo, hi in RUNS:
        quant(v("q0", lo, hi), v("s0", lo, hi), v("X0", 4 * lo, 4 * hi))

    for t in range(R):
        unit = 1.0 if t == R - 1 else float(C)
        for i, (lo, hi) in enumerate(RUNS):
            mm(bank(4 + i, hi - lo), v("uq"), v("us"), v("q%d" % t, lo, hi), v("s%d" % t, lo, hi))
            act(v("sw", lo, hi), bank(4 + i, hi - lo), F.Sign, bias=-1e-36)
        for b in range(4):
            mm(bank(b, C), quad("eq", b, 128), quad("es", b, 128), v("q%d" % t), v("s%d" % t))
            act(v("Dw", 384 * b, 384 * b + C), bank(b, C))
        tt(st("PC", 1, 2, 0, 64), fb("TB", FC), fb("TB", FK), A.add)
        tt(v("A1", 0, 60), fa(0, 0, 60), fa(1, 0, 60), A.add)
        ts(v("offT", 0, 60), v("A1", 0, 60), 192.0, A.add)
        act(v("sm", 0, 4), fa(1, 60, 64), F.Abs, bias=-800.0, scale=2.0)
        tt(v("sm", 4, 8), v("sm", 0, 4), fa(0, 60, 64), A.add)
        double(0, v("sm", 4, 8), 4)
        if t:
            cp(v("offL", 0, 8), v("fl", 0, 8))
            act(v("Zw"), by(v("W3"), v("offL", 0, 8)))
        else:
            ts(v("sm", 48, 52), fa(1, 60, 64), 0.0, A.is_equal, 3.0, A.mult)
            tt(v("sm", 52, 56), v("sm", 48, 52), v("A2", 60, 64), A.add)
            double(8, v("sm", 52, 56), 6)
            cp(v("offL", 0, 16), v("fl", 0, 16))
            act(v("Zw"), by(v("F3w"), v("offL", 8, 16)))
        tr(nd("TBz", ALL), v("Zw"))
        tt(nd("zz", ALL), nd("TBz", ALL, 0, BOTH), nd("TBz", ALL, 1, BOTH), A.add)
        tt(v("sm", 12, 16), nd("zz", ALL, 0), nd("zz", ALL, 1), A.add)
        for h in (0, 1):
            act(nd("lm", ALL, h), v("sm", 12, 16), F.Identity, scale=col(2 + h))
        tt(nd("fc", 0), nd("lm", ALL), nd("d1", ALL), A.add)
        act(st("KB", 0, 2), fb("TB", FC, 0, 60), F.Identity, bias=143360.0, scale=-960.0)
        act(st("KA", 1, 2), fb("TB", FK, 0, 60), F.Identity, scale=-1.0)
        scan(v("PK", 0, 120), v("KA", 0, 120), v("KB", 0, 120), A.add, A.max)
        act(v("b1", 0, 60), fb("TB", FK, 0, 60), F.Abs, bias=-2.5 * unit, scale=2.0 * unit / C)
        for c in range(3):
            act(st("PB", 0, 2, 20 * c, 20 * c + 20), quad("b1", (c + 2) % 3, 20), F.Identity, bias=-unit * (c + 0.5))
        act(st("PA", 0, 4, 20, 60), fb("TB", FC, 0, 40))
        act(st("PA", 0, 4, 0, 20), fb("TB", FC, 40, 60))
        act(v("t2", 0, 40), st("PC", 1, 2, 20, 60))
        act(v("t2", 40, 60), st("PC", 1, 2, 0, 20))
        tt(st("PC", 0, 2), v("t2", 0, 60), st("PC", 1, 2), A.subtract)
        act(st("TQ", 1, 2, 60, 64), st("PC", 1, 2, 60, 64))
        if t == R - 1:
            act(st("U", FK, 16, 60, 64), st("U", FC, 16, 60, 64), F.Identity, scale=-2.0, bias=256.0)
        for b in range(4):
            for c, src in ((0, fa(0, 60, 64)), (1, nd("zz", ALL, 0))):
                act(nd("fc", 1 + b, ALL, c, ALL), src, F.Identity, scale=4.0, bias=768.0 + b)
        if t:
            cp(v("offL", 16, 56), nd("fc", ALL))
        else:
            cp(v("offL", 24, 56), nd("fc", slice(1, 5)))
            cp(v("offL", 16, 24), nd("fc", 0))
        for b in range(4):
            act(v("ct%d" % t, b, 512, 4), by(v("X%d" % t), quad("offL", 3 + b, 8)))
        quant(v("cq%d" % t), v("cs%d" % t), v("ct%d" % t))
        sent = None
        for i, src, rel, land, f in ((0, "cq", "rq", "lq", lambda a: a.bitcast(dt.uint8)), (1, "cs", "rs", "ls", lambda a: a)):
            sent = send([(f(T["%s%d" % (src, t)][:, 64 * side:64 * side + 64]), f(T["%s%d" % (rel, t)][:, 0:64]),
                          f(T["%s%d" % (land, t)][:, 64 - 64 * side:128 - 64 * side])) for side in (0, 1)],
                        ("ac%d" % t, "rc%d" % t), [v("%s%d" % (src, t))], sent, lambda es: _share(es, t, i))
        gather("G1", "TB1", "G1w", v("sw"), "offO", t, 1)
        tr(nd("TBs", ALL), v("sw", 0, C))
        for k in range(3):
            tt(quad("sc", (k + 1) % 3, 20), fb("TBs", t, 0, 20), st("PK", 1, 2, 20 * k, 20 * k + 20), A.mult)
        tt(v("yy", 0, 60), fb("TB1", t, 0, 60), v("sc", 0, 60), A.mult)
        tt(v("yy", 60, 100), fb("TB1", t, 0, 40), v("sc", 0, 40), A.mult)
        tt(v("lo", 0, 60), v("yy", 20, 80), v("yy", 40, 100), A.min)
        ts(v("t9", 0, 60), v("lo", 0, 60), -1.0, A.min)
        tt(fb("TB", 0, 0, 60), v("yy", 0, 60), v("t9", 0, 60), A.is_lt)
        tr(v("C2w", 0, 640), blk("TB", 10, 30))
        tr(v("C2w", 640, 960), blk("TB", 0, 10))
        act(v("Gl", 128, 256), by(v("C2w"), v("offL", 16, 24)), F.Identity, scale=32.0)
        tt(v("Gl", 0, 128), by(v("C2w"), v("offL", 0, 8)), v("Gl", 128, 256), A.mult)
        tr(nd("TBl", ALL), v("Gl", 0, 128))
        tt(v("sm", 24, 28), nd("TBl", ALL, 0, 0), nd("TBl", ALL, 1, 0), A.add)
        cp(v("sl%d" % t), v("sm", 24, 28))
        told = send([(T["sl%d" % t][:, 2 * side:2 * side + 2], T["rl%d" % t][:, 0:2], T["ll%d" % t][:, 2 - 2 * side:4 - 2 * side])
                     for side in (0, 1)], ("al%d" % t, "rl%d" % t), [v("sl%d" % t)], sent, lambda es: es)
        gather("G2", "TB2", "G2w", v("C2w", 0, 1024), "offT", t, 1)
        tt(st("GO", 2, 4, 20, 80), fb("TB2", 0, 0, 60), fb("TB", 0, 0, 60), A.mult)
        tt(st("GO", 2, 4, 0, 20), fb("TB2", 0, 40, 60), fb("TB", 0, 40, 60), A.mult)
        tt(v("ys", 0, 20), fb("TB2", FC, 40, 60), fb("TB2", FK, 40, 60), A.add)
        tt(v("ys", 20, 60), fb("TB2", FC, 0, 40), fb("TB2", FK, 0, 40), A.add)
        gp, gn = v("GO", 80, 320, 2), v("GO", 0, 240, 2)
        for c in range(3):
            act(st("PB", 1, 2, 20 * c, 20 * c + 20), st("GO", 2, 4, 20 * c, 20 * c + 20), F.Identity,
                scale=unit * (-1.0 if c else 2.0), bias=unit * c)
        scan(v("U", FC - 8, 960, 4), v("GO", 80, 320), v("PA"))
        scan(v("U", FK - 8, 960, 8), gp, v("PB"))
        scan(v("PD", 0, 120), gp, v("PC", 0, 120))
        tt(st("PD", 0, 2), v("ys", 0, 60), st("PC", 1, 2), A.subtract)
        scan(v("TQ", 0, 120), gn, v("PD", 0, 120))
        if t != 1:
            tr(v("F3w", 960, 1024), v("U", 960, 1024))
        tr(v("F3w", 0, 960), v("U", 0, 960))
        swap1([v("TQ", 1 + 2 * e, 128, 4) for e in (0, 1)], halves("A2"))
        ts(v("offM"), v("A2"), 192.0, A.add)
        gather("G3", "TB", "W3", v("F3w", 0, 1024), "offM", 1, 0)
        swap2(pair("TB"), twins)
        ts(v("offO", 0, 60), fa(0, 0, 60), 192.0, A.add)
        if t == R - 1:
            for k in range(3):
                act(v("oto", k, 960, 3), v("W3", C * k, C + C * k), F.Identity, bias=col(12), scale=col(11))
            act(v("oto", 960, 1024), v("W3", 960, 1024), F.Identity, bias=col(12), scale=col(11))
            ot = (T.ot[:], [("ot", 1)])
            dma("y", ot, (T.oto[FC:128:16, :], v("oto")[1]), 100000)
            dma("g", ot, (T.oto[FK:128:16, :], v("oto")[1]), 450000, accum_op=A.add)
        for b in range(4):
            mm(bank(4 + b, 128), quad("eq", b, 128), quad("es", b, 128), v("lq%d" % t), v("ls%d" % t),
               ext=("ac%d" % t, 4 * len(_share(eng[0], t, 0)), sent, [p[2][t] for p in PACE]))
            act(quad("Cw", b, 128), bank(4 + b, 128))
            act(v("Dw", 384 * b + C, 384 * b + 384), by(quad("Cw", b, 128), (T["ll%d" % t][:, 0:4], [])),
                ext=("al%d" % t, 16, told, [p[3] for p in PACE]))
        for b in range(4):
            for lo, hi in (((0, C),) if b or t < R - 1 else RUNS):
                (cp if lo else act)(v("p0", C * b + lo, C * b + hi), by(quad("Dw", b, 384), v("offO", lo // 16, hi // 16)))
            tt(quad("tm", b, C), by(quad("Dw", b, 384), v("offO", 20, 40)), quad("p0", b, C), A.max)
        for lo, hi in RUNS:
            n = hi - lo
            for b in range(4):
                tt(v("M%d" % t, 4 * lo + b, 4 * hi, 4), by(quad("Dw", b, 384), v("offO", 40 + lo // 16, 40 + hi // 16)),
                   v("tm", C * b + lo, C * b + hi), A.max)
            mq, ms = v("mq%d" % t, lo, hi), v("ms%d" % t, lo, hi)
            quant(mq, ms, v("M%d" % t, 4 * lo, 4 * hi))
            for b in range(4):
                rr = v("rr", C * b + lo, C * b + hi)
                mm(bank(4 + b, n), quad("wq", b, 128), quad("wsb", b, 128), mq, ms)
                act(rr, bank(4 + b, n), F.Relu, scale=0.015625)
                tt(v("X%d" % (t + 1), 4 * lo + b, 4 * hi, 4), v("ps", 512 * b + lo, 512 * b + hi), rr, A.add)
            q, s = v("q%d" % (t + 1), lo, hi), v("s%d" % (t + 1), lo, hi)
            quant(q, s, v("X%d" % (t + 1), 4 * lo, 4 * hi))
    for i, (lo, hi) in enumerate(RUNS):
        n, q, s = hi - lo, v("q%d" % R, lo, hi), v("s%d" % R, lo, hi)
        mm(bank(4 + i, n), v("vq"), v("vs"), q, s)
        act(v("yb", lo, hi), bank(4 + i, n))
        dma("s" if i else "y", T.y[:, lo:hi], v("yb", lo, hi), 512 * n)
        dma("y", T.oc[:, 4 * lo:4 * hi], raw(q), 512 * n)
    for k in range(4):
        dma("s" if k < 2 else "y", T.osc[4 * k:4 * k + 4, :], (T.s3[32 * k:32 * k + 4, :], v("s3")[1]), 1280)

    known = {q: {} for q in queue}
    count = {}

    def wait(q, sem, n, more):
        if known[q].get(sem, 0) < n:
            queue[q].wait_ge(T.sem[sem], n)
            known[q][sem] = n
            for s in more:
                known[q][s] = max(known[q].get(s, 0), more[s])

    ndma, nsent = 0, 0
    for i in _order(ops):
        o = ops[i]
        q = o["q"]
        for j in sorted(o["deps"], key=lambda j: -ops[j]["at"]):
            wait(q, ops[j]["sem"], ops[j]["cnt"], ops[j]["known"])
        if o["ext"]:
            wait(q, o["ext"][0], o["ext"][1], {})
        ins = o["fn"](*o["args"], **o["kw"])
        if o["kind"] == "r":
            nsent += o["left"]
            continue
        sem, inc = ("c" + q, 1) if o["kind"] == "c" else ("d%d" % ndma, 16)
        ndma += o["kind"] == "d"
        count[sem] = count.get(sem, 0) + inc
        ins.then_inc(T.sem[sem], inc)
        o["sem"], o["cnt"], o["known"] = sem, count[sem], dict(known[q])
    g.wait_ge(T.sem.loc, nsent)
    for sem in count:
        wait("g", sem, count[sem], {})
